import numpy as np, ml_dtypes
CORES = [8,136,40,168]
N = 4
BF = ml_dtypes.bfloat16
def gentries(a):
    return np.ascontiguousarray(a.reshape(8, 16, -1).transpose(0, 2, 1)).reshape(8, -1)
def gtable(e):
    e = np.asarray(e); return np.ascontiguousarray(e.reshape(8, -1, 16).transpose(0, 2, 1)).reshape(128, -1).astype(np.int32)
V, G, R, CAP, L, RO = 1568, 160, 512, 128, 3, 3
W = V + (N - 1) * G
def full(p):
    return np.concatenate([p, np.broadcast_to(np.arange(V, W), (N, 8, W - V))], axis=2).astype(np.int64)
def reach(t, p):
    m = t; q = p
    for i in range(L):
        m = np.maximum(m, np.take_along_axis(m, q[:, :, None, :], 3)); q = np.take_along_axis(q, q, 2)
    return m
def pointers(rng, stay):
    p = rng.integers(0, W, (N, 8, V))
    return np.where(rng.random((N, 8, V)) < stay, np.arange(V), p)
def base(rng):
    x = (256 * rng.random((N, 8, 16, W)) * rng.random((N, 8, 1, W))).astype(np.int32)
    return x, pointers(rng, 0.3), pointers(rng, 0.3), rng.integers(0, W, (N, 8, 16, R)), rng.integers(0, V, (N, 8, N - 1, G))
def both(x, up, lo):
    return reach(x, full(up))[..., :V], reach(x, full(lo))[..., :V]
def witness(rng, mu, ml):
    s = mu.shape; w = np.where(rng.random(s) < rng.random((N, 8, 1, V)), mu, ml) + rng.integers(-6, 7, s)
    w = w + np.where(rng.random((N, 8, 1, V)) < 0.3, rng.integers(-120, 121, s), 0)
    return np.minimum(np.maximum(w, 0), 255)
def bar(mu, ml, w, n):
    d = np.add.reduce(np.abs(mu - w), axis=2) + np.add.reduce(np.abs(ml - w), axis=2)
    return np.take_along_axis(np.sort(d, axis=2), V - 1 - n[:, :, None], 2)[:, :, 0]
def pack(x, w, th, up, lo, rl, snd):
    return {"x": np.ascontiguousarray(x.reshape(N, 128, W)).astype(np.float32).astype(BF), "w": np.ascontiguousarray(w.reshape(N, 128, V)).astype(np.float32).astype(BF),
            "th": np.repeat(th, 16, axis=1).reshape(N, 128, 1).astype(np.int32), "up": np.stack([gtable(a) for a in up]), "lo": np.stack([gtable(a) for a in lo]),
            "rl": np.ascontiguousarray(rl.reshape(N, 128, R)).astype(np.int32), "snd": np.stack([gtable(a.reshape(8, -1)) for a in snd])}
def setup_inputs(rng):
    x, up, lo, rl, snd = base(rng); mu, ml = both(x, up, lo); w = witness(rng, mu, ml)
    n = rng.choice(np.array([CAP // 4, CAP - 8, 2 * CAP, 4 * CAP]), (N, 8))
    return pack(x, w, bar(mu, ml, w, n), up, lo, rl, snd)
def setup_inputs_room(rng):
    x, up, lo, rl, snd = base(rng); mu = reach(x, full(up))[..., :V]
    n = rng.choice(np.array([0, 1, CAP - 1, CAP, CAP + 1, V]), (N, 8)); n[0] = (CAP, CAP + 1, V, CAP - 1, 1, 0, CAP, CAP + 1); n[1, 0] = CAP
    mark = np.argsort(rng.random((N, 8, V)), axis=2) < n[:, :, None]
    off = np.where(mark[:, :, None, :], rng.integers(20, 91, mu.shape), rng.integers(0, 4, mu.shape))
    return pack(x, np.where(mu < 128, mu + off, mu - off), rng.integers(100, 600, (N, 8)), up, up, rl, snd)
def setup_inputs_alike(rng):
    x, up, lo, rl, snd = base(rng); ends = np.array([0, 3, V - 1, V, W - 1])
    x = np.take_along_axis(rng.integers(0, 256, (N, 8, 16, 6)), rng.integers(0, 6, (N, 8, 1, W)), 3).astype(np.int32)
    up = pointers(rng, 0.6); lo = pointers(rng, 0.6)
    up[:, 1::2] = np.where(rng.random((N, 4, V)) < 0.5, rng.choice(ends, (N, 4, V)), up[:, 1::2]); lo[:, ::4] = rng.choice(ends, (N, 2, V))
    rl[:, 2:6] = np.tile(rl[:, 2:6, :4], (1, 1, 4, 1)); rl[:, 6] = rng.choice(ends, (N, 16, R)); rl[:, 7] = rl[:, 7, :1]
    snd[:, ::2] = rng.choice(np.array([0, 3, V - 2, V - 1]), (N, 4, N - 1, G))
    mu, ml = both(x, up, lo); w = witness(rng, mu, ml); n = rng.choice(np.array([CAP // 2, CAP, 2 * CAP]), (N, 8))
    return pack(x, w, bar(mu, ml, w, n), up, lo, rl, snd)
def setup_inputs_deep(rng):
    x, up, lo, rl, snd = base(rng)
    x = (rng.integers(0, 16, x.shape) + np.where(rng.random((N, 8, 1, W)) * 12 < 1, rng.integers(0, 240, x.shape), 0)).astype(np.int32)
    for c in (0, V - 1, V, W - 1): x[..., c] = rng.integers(0, 256, (N, 8, 16))
    up[:, ::2] = (np.arange(V) + 1) % V
    o = np.argsort(rng.random((N, 4, V)), axis=2); p = np.empty_like(o); np.put_along_axis(p, o, np.roll(o, -1, axis=2), 2); up[:, 1::2] = p
    lo = pointers(rng, 0.0); lo[:, ::3] = np.maximum(np.arange(V) - 1, 0); lo[:, 1, V - 1] = W - 1; lo[:, 2, 0] = V
    mu, ml = both(x, up, lo); w = witness(rng, mu, ml); n = rng.choice(np.array([CAP // 2, CAP, 3 * CAP]), (N, 8))
    return pack(x, w, bar(mu, ml, w, n), up, lo, rl, snd)
def setup_inputs_crowd(rng):
    x, up, lo, rl, snd = base(rng); own = np.arange(V); m = np.argsort(rng.random((N, 8, V)), axis=2); w = np.zeros((N, 8, 16, V), np.int64)
    lo[:, :2] = up[:, :2]; mark = own % 16 == rng.integers(0, 16, (N, 2, 1))
    mu = reach(x[:, :2], full(up)[:, :2])[..., :V]
    off = np.where(mark[:, :, None, :], rng.integers(20, 91, mu.shape), rng.integers(0, 4, mu.shape))
    w[:, :2] = np.where(mu < 128, mu + off, mu - off)
    for a in range(N):
        for g in (2, 3, 4, 5, 7):
            b = 37 if g < 4 else 1; n = CAP if g in (2, 7) else int(rng.choice(np.array([CAP, CAP + 1, V // 2])))
            big = np.flatnonzero(m[a, g] >= V - b); hit = m[a, g] < n
            x[a, g] = x[a, g] * 5 // 8; x[a, g][:, big] = rng.integers(201, 256, (16, b))
            if g == 7:
                zero = np.flatnonzero((m[a, g] >= V - 65) & (m[a, g] < V - 1)); x[a, g][:, zero] = 0; rl[a, g] = rng.choice(zero, (16, R))
            lo[a, g] = np.where(hit, rng.choice(big, V), own)
            go = hit & (g < 7)
            up[a, g] = np.where(go & ~np.isin(up[a, g], big), up[a, g], own)
            mine = x[a, g][:, :V]
            w[a, g] = np.where(go, (mine * rng.random(mine.shape)).astype(np.int64), mine)
            if g == 5:
                p = up[a, g].copy(); up[a, g] = lo[a, g]; lo[a, g] = p
    far = np.zeros((N, 8, 1, 1), bool); far[:, 6] = True; far[int(rng.integers(0, N))] = True
    x = np.where(far, 200 + x * 55 // 255, x); w = np.where(far, rng.integers(0, 31, w.shape), w)
    return pack(x, w, rng.integers(100, 600, (N, 8)), up, lo, rl, snd)
def setup_inputs_spread(rng):
    x, up, lo, rl, snd = base(rng)
    cs = np.exp2(8 * rng.random((N, 8, 1, W))) * (rng.random((N, 8, 1, W)) > 0.0625)
    x = np.minimum((cs * rng.random(x.shape)).astype(np.int32), 255)
    up = pointers(rng, rng.choice(np.array([0.0, 0.1, 0.5, 0.9]), (N, 8, 1))); lo = pointers(rng, rng.choice(np.array([0.0, 0.1, 0.5, 0.9]), (N, 8, 1)))
    mu, ml = both(x, up, lo)
    w = np.where(rng.random((N, 8, 1, 1)) < 0.5, witness(rng, mu, ml), np.minimum((cs[..., ::-1][..., :V] * rng.random(mu.shape)).astype(np.int32), 255))
    th = bar(mu, ml, w, rng.choice(np.array([0, 1, CAP, 3 * CAP, V - 1]), (N, 8)))
    th = np.where(rng.random((N, 8)) < 0.2, rng.choice(np.array([0, 8160]), (N, 8)), th)
    return pack(x, w, th, up, lo, rl, snd)
def check_inputs(d):
    bad = []
    for k, least, most in (("x", 0, 255), ("w", 0, 255), ("th", 0, 8160), ("up", 0, W - 1), ("lo", 0, W - 1), ("rl", 0, W - 1), ("snd", 0, V - 1)):
        a = np.asarray(d[k]).astype(np.float64)
        if not (np.min(a) >= least and np.max(a) <= most): bad.append("range of " + k)
        elif np.any(a != np.floor(a)): bad.append("whole numbers in " + k)
    t = np.asarray(d["th"]).reshape(-1, 16)
    if np.any(t != t[:, :1]): bad.append("th alike in a group")
    return bad
def reference(x, w, th, up, lo, rl, snd):
    t = x.astype(np.float32).astype(np.int32).reshape(N, 8, 16, W).copy(); z = w.astype(np.float32).astype(np.int32).reshape(N, 8, 16, V)
    lim = th.astype(np.int64).reshape(N, 8, 16)[:, :, 0]
    hi = full(np.stack([gentries(a) for a in up])); dn = full(np.stack([gentries(a) for a in lo]))
    rh = rl.astype(np.int64).reshape(N, 8, 16, R).copy(); sl = np.stack([gentries(a) for a in snd]).astype(np.int64).reshape(N, 8, N - 1, G)
    last = np.zeros(N, np.int64)
    for rnd in range(RO):
        mu = reach(t, hi); ml = reach(t, dn)
        y = np.concatenate([mu[:, :, :8], ml[:, :, 8:]], axis=2)
        du = np.add.reduce(np.abs(mu[..., :V] - z), axis=2); dl = np.add.reduce(np.abs(ml[..., :V] - z), axis=2)
        bad = du + dl > lim[:, :, None] + (last & 15)[:, None, None]
        last = np.add.reduce(bad.reshape(N, 8 * V).astype(np.int64), axis=1)
        for a in range(N):
            for g in range(8):
                v = np.flatnonzero(bad[a, g])[:CAP]
                if len(v) == 0: continue
                upper = du[a, g, v] >= dl[a, g, v]
                h = np.where(upper, hi[a, g, v], dn[a, g, v]) & (R - 1)
                can = rh[a, g][:, h]
                e = np.add.reduce(np.abs(y[a, g][:, can] - z[a, g][:, v][:, None, :]), axis=0)
                k = np.argmin(e, axis=0); c = can[k, np.arange(len(v))]
                hi[a, g, v[upper]] = c[upper]; dn[a, g, v[~upper]] = c[~upper]
                cls, first = np.unique(h, return_index=True)
                rh[a, g, k[first], cls] = v[first]
        if rnd < RO - 1:
            for a in range(N):
                for d in range(1, N):
                    q = (a - d) % N
                    t[a, :, :, V + (d - 1) * G:V + d * G] = np.take_along_axis(y[q], sl[q, :, d - 1][:, None, :], 2)
    return {"y": np.ascontiguousarray(y[..., :V]).reshape(N, 128, V).astype(np.float32).astype(BF), "up1": np.stack([gtable(a) for a in hi[..., :V]]).astype(np.float32),
            "lo1": np.stack([gtable(a) for a in dn[..., :V]]).astype(np.float32), "rl1": rh.reshape(N, 128, R).astype(np.float32)}

@@ -1,0 +1,610 @@
+from concourse.bass import DstId, RemoteDMATransfer
+from concourse.mybir import AluOpType as A, ActivationFunctionType as F
+
+V, W, NG, NJ, NX, RO = 1568, 2048, 160, 98, 106, 3
+FAR = 3392
+PWW = FAR + V
+BIG = 1048576
+CH = [(0, 32), (32, 60), (60, 82), (82, 98)]
+JA = 60
+H0 = 48
+GV = 64
+KS = ((0, 3, "v"), (1, 3, "s"), (2, 4, "v"), (3, 4, "s"), (6, 2, "v"))
+
+CY, PE, HOP, SAME, REM, FIX = 0.00104, 0.00052, 0.10, 0.06, 6.0, {"v": 0.05, "s": 0.1}
+SCALES = ((1.0, 1.0, 1.0), (0.7, 1.0, 1.2), (1.3, 1.0, 1.0), (1.0, 1.5, 1.2))
+TRIES = 2000
+PLAN = []
+
+BF, FP, I32, U16 = "bfloat16", "float32", "int32", "uint16"
+SB = {
+    "X0": (W, BF), "X1": (W, BF), "X2": (W, BF), "M1U": (W, BF), "M1L": (W, BF), "M2U": (W, BF), "M2L": (W, BF),
+    "C1U": (V, BF), "C1L": (V, BF), "C2U": (V, BF), "C2L": (V, BF), "EK": (128, FP), "KK": (128, BF),
+    "YY": (W, BF), "ML": (V, BF), "WT": (V + 128, BF), "AU": (V, BF), "AL": (V, BF),
+    "PU": (PWW, BF), "PL": (PWW, BF), "P2U": (W, BF), "P2L": (W, BF), "P4U": (V, BF), "P4L": (V, BF),
+    "ULI": (200, I32), "ULA": (196, I32), "PP": (392, BF), "LS": (6 * NJ, U16), "THI": (4, I32), "THR": (4, FP),
+    "BI": (4, I32), "BJ": (4, I32), "RLI": (512, I32), "RLW": (648, FP), "SNI": (32, I32), "SNL": (32, U16),
+    "SB0": (480, BF), "SB1": (480, BF),
+    "UW": (16 * 144, BF), "BB": (4 * 144, BF), "II": (256, BF), "NII": (128, BF), "IDF": (128, FP), "ONE": (256, BF),
+    "NONE": (128, BF), "ONF": (128, FP), "OB": (128, BF), "OBT": (128, BF), "NOB": (128, BF), "OB2": (128, BF),
+    "TRI": (128, BF), "EV": (128, BF), "OD": (128, BF), "ZM": (128, BF),
+    "T8": (24, BF), "BI2": (8, BF), "NBI": (8, BF), "ECI": (848, FP), "EC": (848, BF), "JT": (424, BF), "J16": (112, BF),
+    "N1": (128, FP), "N0": (128, BF), "RST": (128, FP), "RS0": (128, FP), "RS2": (1024, BF), "DD": (1024, BF),
+    "DS": (1024, BF), "C24": (24, FP), "DUM": (8, FP), "NW": (8, FP), "T16": (8, FP), "ENI": (8, I32), "ENL": (8, U16),
+    "PI": (4, I32), "PJ": (4, I32), "COL": (8, FP), "GI": (480, FP),
+    "TU": (NJ, FP), "DUS": (NJ, FP), "DH": (NJ, FP), "HL": (NJ, FP), "BAD": (112, BF), "CUM": (112, BF), "UPP": (NJ, FP),
+    "TT": (NJ, FP), "HS": (112, BF), "FW": (112, BF), "ZW": (112, FP), "SC": (848, FP), "JL": (8, U16), "HJ": (16, BF),
+    "OH": (128, BF), "QQ": (512, BF), "OJ": (128, BF), "LST": (16, U16), "HV": (16, FP), "CL": (128, U16),
+    "WA": (128, BF), "GG": (W, BF), "AA": (W, BF), "QP": (128, BF), "CAB": (256, BF), "CF": (128, FP), "SM": (128, FP),
+    "ST": (128, BF), "M2": (256, BF), "CP": (128, BF), "VUL": (16, U16), "NB": (8, FP), "HN": (8, FP), "XX": (8, FP),
+    "XY": (8, FP), "RLL": (8, U16), "DVC": (128, FP), "TV": (128, FP), "OU": (NJ, FP), "OL": (NJ, FP),
+}
+SCRATCH = {k: ("sbuf", [128, n], d) for k, (n, d) in SB.items()}
+for _b in range(8):
+    SCRATCH["ps%d" % _b] = ("psum", [128, 512], FP)
+NDMA = 44
+SEMAPHORES = ["cv", "cs", "cp", "cg", "arr0", "arr1", "snt0", "snt1", "dy0", "dy1", "dy2"] + ["d%d" % _i for _i in range(NDMA)]
+
+
+def R(name, a=0, b=None, s=1, p0=0, p1=128):
+    return (name, a, SB[name][0] if b is None else b, s, p0, p1)
+
+
+def rank_program(g, core, T, topo):
+    rank = T.rank_of(core)
+    if rank is None:
+        return
+    cores = list(T.cores)
+    n = len(cores)
+    Q = {"v": g.vector, "s": g.scalar, "p": g.tensor, "g": g, "y": g.sync}
+    ops = []
+    ndma = [0]
+
+    def ap(x):
+        if not isinstance(x, tuple):
+            return x
+        if x[0] == "*":
+            return ap(x[1]).indirect(ap(x[2]))
+        if x[3] != 1:
+            return T[x[0]][:, x[1]:x[2]:x[3]]
+        if x[5] - x[4] < 128:
+            return T[x[0]][x[4]:x[5], x[1]:x[2]]
+        return T[x[0]][:, x[1]:x[2]]
+
+    def IX(win, off):
+        return ("*", win, off)
+
+    def width(x):
+        return 16 * width(x[2]) if x[0] == "*" else len(range(x[1], x[2], x[3]))
+
+    def narrow(*xs):
+        return all(x[0] in SB and SB[x[0]][1] in (BF, U16) for x in xs)
+
+    def cost(q, outs, ins, f):
+        o, i = outs[0], ins[0] if ins else None
+        if q == "p":
+            return max(64, width(o)) * PE * (4 if SB[i[0]][1] == FP else 1)
+        if q == "g":
+            return 0.15 + 2 * width(o) * CY
+        if o[0] == "*":
+            return FIX[q] + width(o) * 3.8 * CY
+        if i is not None and i[0] == "*":
+            return FIX[q] + width(o) * 1.56 * CY
+        if f is None:
+            f = 0.5 if q == "v" and narrow(o, *[x for x in ins if isinstance(x, tuple) and width(x) > 1]) else 1
+        return FIX[q] + max(64, width(o) * f) * CY
+
+    def add(q, fn, outs, ins, sem=None, inc=1, free=False, pre=None, f=None, lat=0.0, post=None, after=()):
+        rd, wr = [], []
+        for x in ins:
+            if isinstance(x, tuple):
+                rd.extend([x[1], x[2]] if x[0] == "*" else [x])
+        for x in outs:
+            if x[0] == "*":
+                wr.append(x[1])
+                rd.append(x[2])
+            else:
+                wr.append(x)
+        ops.append({"q": q, "fn": fn, "rd": rd, "wr": wr, "sem": sem or "c" + q, "inc": inc, "free": free, "pre": pre, "post": post,
+                    "cost": (0.1 if inc else 1.0) if free else cost(q, outs, ins, f), "lat": lat, "deps": set(after), "order": set(),
+                    "ix": any(isinstance(x, tuple) and x[0] == "*" for x in list(outs) + list(ins))})
+        return len(ops) - 1
+
+    def cp(o, i):
+        return add("v", lambda: g.vector.tensor_copy(ap(o), ap(i)), [o], [i])
+
+    def tt(o, a, b, op):
+        return add("v", lambda: g.vector.tensor_tensor(ap(o), ap(a), ap(b), op), [o], [a, b], f=1 if "ps" in (a[0][:2], b[0][:2]) else 2)
+
+    def ts(o, a, s1, op0, s2=None, op1=None):
+        if op1 is None:
+            return add("v", lambda: g.vector.tensor_scalar(ap(o), ap(a), ap(s1), None, op0), [o], [a, s1])
+        return add("v", lambda: g.vector.tensor_scalar(ap(o), ap(a), ap(s1), ap(s2), op0, op1), [o], [a, s1, s2])
+
+    def scan(o, d0, d1, init, op0, op1):
+        return add("v", lambda: g.vector.tensor_tensor_scan(ap(o), ap(d0), ap(d1), init, op0, op1), [o], [d0, d1])
+
+    def mset(o, c):
+        return add("v", lambda: g.vector.memset(ap(o), c), [o], [])
+
+    def act(o, i, f=F.Identity, bias=0.0, scale=1.0):
+        return add("s", lambda: g.scalar.activation(ap(o), ap(i), f, bias=ap(bias), scale=ap(scale)), [o], [i, bias, scale])
+
+    def mms(ms):
+        def fn():
+            return [g.tensor.matmul(ap(o), ap(l), ap(r), start, stop) for o, l, r, start, stop in ms][-1]
+        i = add("p", fn, [m[0] for m in ms], [m[1] for m in ms] + [m[2] for m in ms], lat=0.05)
+        ops[i]["cost"] = sum(cost("p", [m[0]], [m[1]], None) for m in ms)
+        return i
+
+    def mm(o, l, r, start, stop):
+        return mms([(o, l, r, start, stop)])
+
+    def iota(o, pat, base, cm=0):
+        if SB[o[0]][1] == I32:
+            add("g", lambda: g.iota(ap(o), pat, base, cm), [o], [])
+        else:
+            add("g", lambda: g.iota(ap(o), pat, base, cm, allow_small_or_imprecise_dtypes=True), [o], [])
+
+    def fill(o, c):
+        iota(o, [[0, width(o)]], c)
+
+    def sel(o, i, pat, op, base, cm, fillv=0.0):
+        add("g", lambda: g.affine_select(ap(o), ap(i), pat, op, fillv, base, cm), [o], [i])
+
+    def dma(q, o, i, pre=None, after=(), s=None):
+        z = o if isinstance(o, tuple) else i
+        if s is None:
+            s = "d%d" % ndma[0]
+            ndma[0] += 1
+        return add(q, lambda: Q[q].dma_start(ap(o), ap(i)), [o] if isinstance(o, tuple) else [], [i], sem=s, inc=16, free=True, pre=pre,
+                   lat=2.0 + width(z) * (0.0012 if narrow(z) else 0.0024) * (z[5] - z[4] + 32) / 160, after=after)
+
+    def chain(ids):
+        for a, b in zip(ids, ids[1:]):
+            ops[b]["order"].add(a)
+
+    def PS(b, a, e, s=1):
+        return ("ps%d" % b, a, e, s, 0, 128)
+
+    def BR(m, r):
+        return R("BB", 144 * m + 15 - r, 144 * m + 143 - r)
+
+    def UWs(r, i):
+        return R("UW", 144 * r + 15 - i, 144 * r + 143 - i)
+
+    def wrap(out, lhs, src, a, b, first=True, last=True):
+        return mms([(out, lhs(r), R(src, a + r, b, 16), first and r == 0, last and r == 15) for r in range(16)])
+
+    def LS(k, a=0, b=NJ):
+        return R("LS", NJ * k + a, NJ * k + b)
+
+    I_, NI_ = R("II", 0, 128), R("NII")
+
+    d0 = dma("y", R("ULI", 0, 98), T.up[:, :])
+    dma("s", R("ULI", 100, 198), T.lo[:, :])
+    dx = dma("y", R("X0"), T.x[:, :])
+    chain([d0, dx, dma("y", R("X1", 0, 16 * H0), T.x[:, 0:16 * H0]), dma("y", R("X1", 16 * H0, V), T.x[:, 16 * H0:V])])
+    for b in ("M1U", "M1L", "M2U", "M2L", "YY"):
+        dma("y", R(b, V, W), T.x[:, V:W], after=[dx])
+    dma("y", R("WT", 0, V), T.w[:, :], after=[dx])
+    dma("y", R("THI", 0, 1), T.th[:, :], after=[dx])
+    dma("y", R("RLI"), T.rl[:, :], after=[dx])
+    dma("y", R("SNI", 0, 30), T.snd[:, :], after=[dx])
+    dma("y", R("X2", 0, V), T.x[:, 0:V], after=[dx])
+
+    fill(R("ONE"), 1)
+    iota(R("PI", 0, 1), [[0, 1]], 0, 1)
+    mset(R("UW"), 0.0)
+    mset(R("BB"), 0.0)
+    sel(R("UW", 15, 2304, 16), R("ONE", 0, 144), [[-1, 16], [-16, 9]], A.is_equal, 0, 1)
+    iota(R("GI"), [[1, 480]], V - 1792)
+    ts(R("PJ", 0, 1), R("PI", 0, 1), 15, A.bitwise_and)
+    ts(R("PJ", 1, 2), R("PI", 0, 1), 1, A.bitwise_and)
+    cp(R("COL", 0, 1), R("PJ", 0, 1))
+    ts(R("COL", 1, 2), R("PJ", 0, 1), 256.0, A.mult)
+    ts(R("COL", 2, 3), R("PJ", 1, 2), -1.0, A.mult, 1.0, A.add)
+    ts(R("COL", 3, 4), R("PJ", 1, 2), 1792.0, A.mult)
+    ts(R("PU", V, W), R("GI"), R("COL", 2, 3), A.mult, R("COL", 3, 4), A.add)
+    cp(R("P2U", V, W), R("PU", V, W))
+    cp(R("P2L", V, W), R("PU", V, W))
+    for m, (lo_, hi_) in ((1, (0, 1)), (2, (2, 3)), (0, (0, 15))):
+        sel(R("T8", 8 * m, 8 * m + 8), R("ONE", 0, 8), [[-16, 8]], A.is_ge, -lo_, 1)
+        sel(R("BB", 144 * m + 15, 144 * m + 128, 16), R("T8", 8 * m, 8 * m + 8), [[16, 8]], A.is_ge, hi_, -1)
+    fill(R("NONE"), -1)
+    sel(R("BB", 144 * 3 + 15, 144 * 3 + 128, 16), R("NONE", 0, 8), [[-16, 8]], A.is_equal, -2, 1)
+    sel(R("II"), R("ONE"), [[0, 2], [-1, 128]], A.is_equal, 0, 1)
+    sel(R("NII"), R("NONE"), [[-1, 128]], A.is_equal, 0, 1)
+    iota(R("ECI"), [[4096, 8], [0, NX]], 128)
+    sel(R("OBT"), R("ONE", 0, 128), [[-16, 8], [0, 16]], A.is_ge, 0, 1)
+    sel(R("OB"), R("OBT"), [[16, 8], [0, 16]], A.is_ge, 15, -1)
+    sel(R("OBT"), R("OB"), [[1, 128]], A.is_gt, 0, -1)
+    sel(R("TRI"), R("OB"), [[1, 128]], A.is_ge, 0, -1)
+    tt(R("TRI"), R("TRI"), R("OBT"), A.add)
+    fill(R("BAD", NJ, 112), 1)
+    fill(R("CUM", 0, 1), 0)
+    fill(R("HS", NJ, 112), 256)
+    fill(R("FW", NJ, 112), FAR // 2)
+    fill(R("HJ", 0, 8), 256)
+    iota(R("JT"), [[0, 4], [1, NX]], 0)
+    iota(R("N1"), [[2, 128]], 1)
+    fill(R("ZM"), 0)
+    fill(R("WT", V, V + 128), 0)
+    fill(R("RLW", 512, 648), 0)
+    iota(R("T16"), [[16, 8]], 0)
+    iota(R("ENI"), [[16, 8]], 15)
+    iota(R("J16"), [[16, 112]], 0)
+    iota(R("N0"), [[1, 128]], 0)
+    fill(R("RS0"), -BIG)
+    sel(R("RST"), R("RS0"), [[0, 8], [1, 16]], A.not_equal, 0, 0, float(BIG))
+    iota(R("KK"), [[0, 8], [1, 16]], 0)
+    sel(R("EV"), R("OB"), [[0, 64], [1, 2]], A.is_equal, 0, 0)
+    sel(R("OD"), R("OB"), [[0, 64], [1, 2]], A.not_equal, 0, 0)
+    fill(R("ONF"), 1)
+    sel(R("IDF"), R("ONF"), [[-1, 128]], A.is_equal, 0, 1)
+    fill(R("C24", 8, 16), 0)
+    fill(R("C24", 16, 24), FAR)
+    fill(R("DD"), BIG)
+    fill(R("RS2"), 0)
+    fill(R("RS2", 0, 1024, 128), BIG)
+    cp(R("THR", 0, 1), R("THI", 0, 1))
+    cp(R("RLW", 0, 512), R("RLI"))
+    cp(R("SNL", 0, 30), R("SNI", 0, 30))
+    cp(R("ENL"), R("ENI"))
+    act(R("EC"), R("ECI"), bias=R("COL", 1, 2))
+    act(R("NOB"), R("OB"), F.Copy, scale=-256.0)
+    act(R("OB2"), R("OB"), F.Copy, scale=256.0)
+    act(R("BI2"), R("OB", 0, 128, 16), F.Copy, scale=32.0)
+    act(R("NBI"), R("OB", 0, 128, 16), F.Copy, scale=-16.0)
+    act(R("NW"), R("T16"), bias=R("COL", 0, 1))
+    act(R("C24", 0, 8), R("NW"), F.Copy, scale=1024.0)
+    act(R("DUM"), R("NW"), bias=513.0)
+
+    cp(LS(0), R("ULI", 0, 98))
+    cp(LS(1), R("ULI", 100, 198))
+    for t in range(2):
+        ts(R("ULA", 98 * t, 98 * t + 98), R("ULI", 100 * t, 100 * t + 98), 511, A.bitwise_and)
+    ts(R("PP", 0, 196), R("ULA"), -256.0, A.add)
+    for t in range(2):
+        tt(R("PP", 196 + 98 * t, 294 + 98 * t), R("ULI", 100 * t, 100 * t + 98), R("PP", 98 * t, 98 * t + 98), A.subtract)
+    ids = []
+    for r in range(16):
+        parts = ((0, 0), (2, 98), (1, 196), (3, 294))
+        ids.append(mms([(PS(r % 8, 0, NJ), UWs(r, i), R("PP", a, a + NJ), i == 0, i == 3) for i, a in parts]))
+        act(R("PU", r, V, 16), PS(r % 8, 0, NJ), F.Copy)
+    chain(ids)
+    dma("y", R("PL", 0, W), R("PU", 0, W))
+
+    for rnd in range(RO):
+        X, XO = "X%d" % rnd, "X%d" % ((rnd + 1) % RO)
+        PLw = "PU" if rnd == 0 else "PL"
+        last = rnd == RO - 1
+        steps, pgs = [], []
+
+        def step(o, win, own, k, a, b):
+            steps.append(tt(R(o, 16 * a, 16 * b), IX(R(win), LS(k, a, b)), R(own, 16 * a, 16 * b), A.max))
+            if rnd and win == X:
+                ops[-1]["pre"] = ("arr%d" % (rnd - 1), 16)
+
+        def step2(o, win, own, k, twin, halves):
+            for h, (a, b) in enumerate(halves):
+                step(o, win, own, k, a, b)
+                if h == 0:
+                    dma("y", R(twin, 16 * a, 16 * b), R(o, 16 * a, 16 * b))
+                else:
+                    sel(R(twin, 16 * a, 16 * b), R(o, 16 * a, 16 * b), [[0, 16 * (b - a)]], A.is_ge, 0, 0)
+
+        def pg(o, win, k):
+            pgs.append(act(R(o, 0, V), IX(R(win, 0, W), LS(k)), F.Copy))
+
+        def far(buf, out, c):
+            a, b = CH[c]
+            mm(PS(c, 0, 16 * (b - a)), I_, R(buf, 16 * a, 16 * b), False, True)
+            act(R(out, 16 * a, 16 * b), PS(c, 0, 16 * (b - a)), F.Abs)
+
+        def negw(c):
+            a, b = CH[c]
+            mm(PS(c, 0, 16 * (b - a)), NI_, R("WT", 16 * a, 16 * b), True, False)
+
+        up_, dn_ = ((0, H0), (H0, NJ)), ((H0, NJ), (0, H0))
+        step2("M1U", X, XO, 0, "C1U", up_)
+        pg("P2U", "PU", 0)
+        step2("M1L", X, XO, 1, "C1L", up_)
+        pg("P2L", PLw, 1)
+        wrap(PS(6, 0, NJ), lambda r: UWs(0, r), "PU", 0, V, True, False)
+        wrap(PS(6, 0, NJ), lambda r: BR(3, r), PLw, 0, V, False, True)
+        wrap(PS(7, 0, NJ), lambda r: UWs(2, r), PLw, 0, V)
+        wrap(PS(4, 0, NJ), lambda r: BR(1, r), "P2U", 0, V)
+        cp(LS(2), PS(4, 0, NJ))
+        step2("M2U", "M1U", "C1U", 2, "C2U", dn_)
+        wrap(PS(5, 0, NJ), lambda r: BR(2, r), "P2L", 0, V)
+        pg("P4U", "P2U", 2)
+        cp(LS(3), PS(5, 0, NJ))
+        step2("M2L", "M1L", "C1L", 3, "C2L", dn_)
+        pg("P4L", "P2L", 3)
+        wrap(PS(4, 0, NJ), lambda r: BR(1, r), "P4U", 0, V)
+        cp(LS(4), PS(4, 0, NJ))
+        wrap(PS(5, 0, NJ), lambda r: BR(2, r), "P4L", 0, V)
+        cp(LS(5), PS(5, 0, NJ))
+        act(R("DH"), PS(6, 0, NJ), F.Copy)
+        act(R("HL"), PS(7, 0, NJ), F.Copy)
+        for h in range(2):
+            mm(PS(6 + h, 0, 424), I_, R("EC", 424 * h, 424 * h + 424), True, False)
+        for c, (a, b) in enumerate(CH):
+            negw(c)
+            step("YY", "M2U", "C2U", 4, a, b)
+            far("YY", "AU", c)
+        wrap(PS(4, 0, JA), lambda r: BR(0, r), "AU", 0, 16 * JA)
+        wrap(PS(4, JA, NJ), lambda r: BR(0, r), "AU", 16 * JA, V)
+        act(R("TU"), PS(4, 0, NJ), bias=R("THR", 0, 1), scale=-1.0)
+        act(R("DUS"), PS(4, 0, NJ), F.Copy)
+        for c, (a, b) in enumerate(CH):
+            negw(c)
+            step("ML", "M2L", "C2L", 5, a, b)
+            far("ML", "AL", c)
+        wrap(PS(5, 0, JA), lambda r: BR(0, r), "AL", 0, 16 * JA)
+        wrap(PS(0, JA, NJ), lambda r: BR(0, r), "AL", 16 * JA, V)
+        chain(steps)
+        chain(pgs)
+        for k in range(8):
+            dma("y", R("YY", 0, V, 1, 16 * k + 8, 16 * k + 16), R("ML", 0, V, 1, 16 * k + 8, 16 * k + 16), s="dy%d" % rnd)
+        if last:
+            dma("y", T.y[:, :], R("YY", 0, V))
+        for a, b, dl in ((0, JA, PS(5, 0, JA)), (JA, NJ, PS(0, JA, NJ))):
+            tt(R("BAD", a, b), dl, R("TU", a, b), A.is_gt)
+            tt(R("UPP", a, b), dl, R("DUS", a, b), A.is_le)
+            tt(R("TT", a, b), R("UPP", a, b), R("DH", a, b), A.mult)
+            tt(R("HS", a, b), R("TT", a, b), R("HL", a, b), A.add)
+        scan(R("CUM", 1, NX + 1), R("BAD", 0, NX), R("BAD", 0, NX), 0.0, A.add, A.max)
+        chain([mms([(PS(6 + h, NX * t, NX * (t + 1)), R("NOB"), R("CUM", 1, NX + 1), False, t == 3) for t in range(4)]) for h in range(2)])
+        mms([(PS(1, 0, NX), R("OB"), R("CUM", 0, NX), True, False), (PS(1, 0, NX), R("OB"), R("CUM", 0, NX), False, False),
+             (PS(1, 0, NX), R("TRI"), R("BAD", 0, NX), False, True)])
+        act(R("ZW", 0, NX), PS(1, 0, NX), F.Copy)
+        for h in range(2):
+            scan(R("SC", 424 * h, 424 * h + 424), R("JT"), PS(6 + h, 0, 424), 1000.0, A.min, A.max)
+        cp(R("JL"), R("SC", NX - 1, 848, NX))
+        act(R("HJ", 8, 16), R("SC", NX - 1, 848, NX), F.Copy, scale=16.0)
+        for c, nk, q in KS:
+            mm(PS(c, 0, 128 * nk), R("ZM"), R("WT", 0, 128 * nk), True, False)
+        mm(PS(4, 256, 384), I_, R("KK"), True, False)
+        tt(R("OH"), IX(R("ZW", 0, NX), R("JL")), R("N1"), A.is_equal)
+        act(R("QQ", 128, 256), R("OH"), F.Copy, scale=R("COL", 0, 1))
+        tt(R("QQ", 0, 128), IX(R("HS", 0, NX), R("JL")), R("OH"), A.mult)
+        mm(PS(5, 128, 144), I_, R("HJ"), True, False)
+        wrap(PS(5, 128, 144), lambda r: BR(0, r), "QQ", 0, 256, False, True)
+        act(R("FW", 0, NJ), R("UPP"), bias=float(FAR), scale=-float(FAR))
+        tt(R("OJ"), IX(R("J16", 0, NX), R("JL")), R("OH"), A.mult)
+        tt(R("QQ", 256, 384), IX(R("FW", 0, NX), R("JL")), R("OH"), A.mult)
+        cp(R("LST"), PS(5, 128, 144))
+        hl, vl = R("LST", 0, 8), R("LST", 8, 16)
+        if not last:
+            act(R("SB%d" % rnd), IX(R("YY"), R("SNL", 0, 30)), F.Copy)
+
+            def send(rnd=rnd):
+                tr = []
+                for d in (1, 2, 3):
+                    dst = cores[(rank + d) % n]
+                    rid, pid = topo.addr(dst, core)
+                    e = topo.engines(core, dst)
+                    hlf = len(e) // 2
+                    e = e[:hlf] if d == 1 else (e[hlf:2 * hlf] if d == 2 else e)
+                    tr.append(RemoteDMATransfer(
+                        dst_ids=[DstId(rid=rid, pnc=pid)], dma_engine_mask=sum(1 << x for x in e), remote_sem=T.sem["arr%d" % rnd],
+                        src=ap(R("SB%d" % rnd, NG * (d - 1), NG * d)), dst=ap(R("X%d" % (rnd + 1), V + NG * (d - 1), V + NG * d))))
+                g.remote_dma_fused(tr[:2], local_sem=T.sem["snt%d" % rnd])
+                g.remote_dma_fused(tr[2:], local_sem=T.sem["snt%d" % rnd])
+                return None
+            add("g", send, [], [R("SB%d" % rnd)], free=True, inc=0, lat=REM, post="arr%d" % rnd)
+        cp(R("CL"), IX(R("RLW"), hl))
+        act(R("WA"), IX(R("WT"), vl), F.Copy)
+        cp(R("GG", 0, 16 * GV), IX(R("YY"), R("CL", 0, GV)))
+        act(R("GG", 16 * GV, W), IX(R("YY"), R("CL", GV, 128)), F.Copy)
+        if not last:
+            for b in ("M1U", "M1L", "M2U", "M2L", "YY"):
+                dma("y", R(b, V, W), R("X%d" % (rnd + 1), V, W), pre=("arr%d" % rnd, 16))
+        ids, k0 = [], 0
+        for c, nk, q in KS:
+            mms([(PS(c, 128 * k, 128 * k + 128), NI_, R("WA"), False, False) for k in range(nk)])
+            ids.append(mms([(PS(c, 128 * k, 128 * k + 128), I_, R("GG", k0 + k, W, 16), False, k == nk - 1) for k in range(nk)]))
+            k0 += nk
+        ids.append(mms([(PS(4, 256 + k, 384, 16), R("GG", k, W, 16), R("NBI"), False, False) for k in range(16)]))
+        chain(ids)
+        act(R("QP"), IX(R("RLW"), hl), bias=191.5009765625, scale=1.0 / 512)
+        k0 = 0
+        for c, nk, q in KS:
+            if q == "s":
+                act(R("AA", 128 * k0, 128 * (k0 + nk)), PS(c, 0, 128 * nk), F.Relu)
+            else:
+                ts(R("AA", 128 * k0, 128 * (k0 + nk)), PS(c, 0, 128 * nk), 0.0, A.max)
+            mms([(PS(4, 256 + k, 384, 16), R("AA", 128 * k, 128 * k + 128), R("BI2"), False, k == 15) for k in range(k0, k0 + nk)])
+            k0 += nk
+        act(R("CAB", 128, 256), R("QP"), bias=-98048.0, scale=512.0)
+        act(R("HV"), PS(5, 128, 144), F.Copy)
+        act(R("QQ", 384, 512), R("QQ", 256, 384), F.Copy, scale=-1.0)
+        scan(R("SM"), R("RST"), PS(4, 256, 384), 0.0, A.max, A.min)
+        cp(R("EK"), PS(4, 256, 384))
+        tt(R("ST"), IX(R("SM"), R("ENL")), R("EK"), A.is_equal)
+        mms([(PS(7, 0, 24), R("IDF"), R("C24"), True, False), (PS(7, 0, 16), R("IDF"), R("HV"), False, False),
+             (PS(7, 16, 24), R("IDF"), R("HV", 8, 16), False, False)])
+        mms([(PS(5, 256, 384), I_, R("N0"), True, False), (PS(5, 256, 384), R("OB2"), R("QQ", 0, 128), False, True)])
+        mm(PS(0, 0, 256), R("ST"), R("II"), True, True)
+        wrap(PS(7, 8, 24), lambda r: BR(0, r), "QQ", 256, 512, False, True)
+        tt(R("CAB", 0, 128), IX(R("RLW"), hl), R("CAB", 128, 256), A.subtract)
+        act(R("NB"), R("HV", 0, 8), bias=67108864.0, scale=-262144.0)
+        act(R("CF"), IX(R("RLW"), hl), F.Copy)
+        tt(R("M2"), PS(0, 0, 256), R("CAB"), A.mult)
+        mms([(PS(1, 0, 128), R("EV"), R("M2", 0, 128), True, False), (PS(1, 0, 128), R("OD"), R("M2", 128, 256), False, True)])
+        mms([(PS(2, 0, 128), R("OB"), R("OJ"), True, False), (PS(2, 0, 128), R("OB"), R("QQ", 128, 256), False, False),
+             (PS(2, 0, 128), NI_, R("CAB", 0, 128), False, False), (PS(2, 0, 128), NI_, R("CAB", 128, 256), False, True)])
+        cp(R("VUL"), PS(7, 8, 24))
+        act(R("HN"), PS(7, 0, 8), F.Copy)
+        cp(R("CP"), PS(1, 0, 128))
+        act(R("DVC"), PS(2, 0, 128), F.Copy)
+        for t in range(8):
+            w_ = 16 * (t + 1)
+            act(R("DD", 128 * t, 128 * t + w_), PS(5, 256, 256 + w_), F.Abs, bias=R("NB", t, t + 1), scale=1024.0)
+        cp(IX(R("PU"), R("VUL", 0, 8)), R("CP"))
+        wrap(PS(4, 0, NJ), lambda r: BR(1, r), "PU", 0, V)
+        cp(IX(R("PL"), R("VUL", 8, 16)), R("CP"))
+        wrap(PS(5, 0, NJ), lambda r: BR(2, r), "PL", 0, V)
+        tt(R("TV"), PS(0, 0, 128), R("DVC"), A.mult)
+        scan(R("DS"), R("RS2"), R("DD"), 0.0, A.max, A.min)
+        tt(R("XX"), R("HN"), R("DS", 127, 1024, 128), A.subtract)
+        tt(R("XY"), R("XX"), R("DUM"), A.min)
+        cp(R("RLL"), R("XY"))
+        tt(IX(R("RLW"), R("RLL")), R("TV"), R("CF"), A.add)
+        if not last:
+            mm(PS(3, 0, 1), R("ONE", 0, 128), R("CUM", NJ, NJ + 1), True, True)
+            cp(LS(0), PS(4, 0, NJ))
+            cp(LS(1), PS(5, 0, NJ))
+            cp(R("BI", 0, 1), PS(3, 0, 1))
+            ts(R("BJ", 0, 1), R("BI", 0, 1), 15, A.bitwise_and)
+            tt(R("THR", 0, 1), R("BJ", 0, 1), R("THI", 0, 1), A.add)
+        else:
+            dma("y", T.rl1[:, :], R("RLW", 0, 512))
+            act(R("OU"), PS(4, 0, NJ), F.Copy)
+            dma("s", T.up1[:, :], R("OU"))
+            act(R("OL"), PS(5, 0, NJ), F.Copy)
+            dma("s", T.lo1[:, :], R("OL"))
+
+    def meet(x, z):
+        if x[1] >= z[2] or z[1] >= x[2] or x[4] >= z[5] or z[4] >= x[5]:
+            return False
+        return not (x[3] == z[3] > 1 and (x[1] - z[1]) % x[3])
+
+    acc, posts = {}, {}
+    for i, o in enumerate(ops):
+        for lst, isw in ((o["rd"], False), (o["wr"], True)):
+            for x in lst:
+                for (j, z, w_) in acc.get(x[0], ()):
+                    p = ops[j]
+                    if x[0][:2] == "ps" and p["q"] != o["q"]:
+                        o["deps"].add(j)
+                    elif x[0][:2] == "ps" and o["q"] == "p":
+                        o["order"].add(j)
+                    elif (w_ or isw) and meet(x, z):
+                        o["deps"].add(j)
+        if o["pre"]:
+            o["order"].add(posts[o["pre"][0]])
+        if o["post"]:
+            posts[o["post"]] = i
+        for lst, isw in ((o["rd"], False), (o["wr"], True)):
+            for x in lst:
+                if x[0][:2] == "ps" and o["q"] == "p":
+                    acc[x[0]] = [e for e in acc.get(x[0], ()) if ops[e[0]]["q"] != "p"]
+                acc.setdefault(x[0], []).append((i, x, isw))
+
+    def delay(p, o, j):
+        if j not in o["deps"] and not p["post"]:
+            return 0.0
+        return p["lat"] + (SAME if p["q"] == o["q"] else HOP)
+
+    every = range(len(ops))
+    pred = [[(j, delay(ops[j], o, j)) for j in sorted(o["deps"] | o["order"])] for o in ops]
+    succ = [[] for o in ops]
+    for i in every:
+        for j, d in pred[i]:
+            succ[j].append((i, d))
+
+    def judge(pri):
+        left = [len(p) for p in pred]
+        ready = [i for i in every if not left[i]]
+        busy, at = {q: [] for q in Q}, {}
+        while ready:
+            i = max(ready, key=lambda j: pri[j])
+            ready.remove(i)
+            c = ops[i]["cost"]
+            t = max([at[j] + ops[j]["cost"] + d for j, d in pred[i]] + [0.0])
+            bz = busy[ops[i]["q"]]
+            k = len(bz)
+            while k and bz[k - 1][1] > t:
+                k -= 1
+            while k < len(bz) and bz[k][0] < t + c - 1e-9:
+                t = max(t, bz[k][1])
+                k += 1
+            bz.insert(k, (t, t + c))
+            at[i] = t
+            for j, d in succ[i]:
+                left[j] -= 1
+                if not left[j]:
+                    ready.append(j)
+        seq = sorted(every, key=lambda i: (at[i], i))
+        return sum(span(seq, sc) for sc in SCALES), seq, at
+
+    def span(seq, scale):
+        at, q_at = {}, {q: 0.0 for q in Q}
+        for i in seq:
+            o = ops[i]
+            t = q_at[o["q"]]
+            for j, d in pred[i]:
+                u = at[j] + (d * scale[2] if ops[j]["free"] else d)
+                if u > t:
+                    t = u
+            at[i] = q_at[o["q"]] = t + o["cost"] * (scale[0] if o["ix"] else scale[1] if o["q"] == "p" else 1.0)
+        return max(at[i] + ops[i]["lat"] for i in every)
+
+    if not PLAN:
+        pri = [o["cost"] + o["lat"] for o in ops]
+        for i in reversed(every):
+            for j, d in pred[i]:
+                pri[j] = max(pri[j], ops[j]["cost"] + d + pri[i])
+        best = judge(pri)
+        z = 12345
+        for _ in range(TRIES):
+            new = list(pri)
+            z = (z * 1103515245 + 12345) % 2147483648
+            a = z // 7 % len(ops)
+            z = (z * 1103515245 + 12345) % 2147483648
+            w_ = 1 + z // 11 % 6
+            z = (z * 1103515245 + 12345) % 2147483648
+            d = (z // 13 % 2001 - 1000) / 1000.0
+            for k in range(a, min(a + w_, len(ops))):
+                new[k] += 2.5 * d * abs(d)
+            got = judge(new)
+            if got[0] <= best[0]:
+                pri, best = new, got
+        PLAN.append(best)
+    seq, at = PLAN[0][1], PLAN[0][2]
+
+    used = set()
+    for o in ops:
+        used |= o["deps"]
+    cnt = {}
+    for i in seq:
+        o = ops[i]
+        o["sig"] = o["inc"] > 0 and (i in used or o["free"])
+        if o["sig"]:
+            cnt[o["sem"]] = cnt.get(o["sem"], 0) + o["inc"]
+            o["val"] = cnt[o["sem"]]
+    for o in ops:
+        if o["free"] and o["sig"]:
+            o["val"] = cnt[o["sem"]]
+    known = {q: {} for q in Q}
+    waited = {}
+    for i in seq:
+        o = ops[i]
+        kn = known[o["q"]]
+        need = {}
+        for j in o["deps"]:
+            p = ops[j]
+            if p["val"] > need.get(p["sem"], (0, 0))[0]:
+                need[p["sem"]] = (p["val"], j)
+        for s, (val, j) in sorted(need.items(), key=lambda z: -at[z[1][1]]):
+            if kn.get(s, 0) < val:
+                Q[o["q"]].wait_ge(T.sem[s], val)
+                waited[s] = max(waited.get(s, 0), val)
+                kn[s] = val
+                for s2, v2 in ops[j]["kn"].items():
+                    if kn.get(s2, 0) < v2:
+                        kn[s2] = v2
+        if o["pre"] and kn.get(o["pre"][0], 0) < o["pre"][1]:
+            Q[o["q"]].wait_ge(T.sem[o["pre"][0]], o["pre"][1])
+            kn[o["pre"][0]] = o["pre"][1]
+        o["kn"] = dict(kn)
+        ins = o["fn"]()
+        if o["sig"]:
+            ins.then_inc(T.sem[o["sem"]], o["inc"])
+    cnt["snt0"] = cnt["snt1"] = 16
+    for s, val in cnt.items():
+        if waited.get(s, 0) < val:
+            g.wait_ge(T.sem[s], val)

@@ -2,18 +2,28 @@ from concourse.bass import DstId, RemoteDMATransfer
 from concourse.mybir import AluOpType as A, ActivationFunctionType as F
 
 V, W, NG, NJ, NX, RO = 1568, 2048, 160, 98, 106, 3
-FAR = 3392
-PWW = FAR + V
+SPARE = 2 * W - V
 BIG = 1048576
-CH = [(0, 32), (32, 60), (60, 82), (82, 98)]
-JA = 60
+CU = ((0, 28, 0), (28, 54, 1), (54, 78, 2), (78, 98, 3))
+CW = ((0, 28, 6), (28, 56, 7), (56, 80, 0), (80, 98, 1))
+JU, JA = 54, 56
 H0 = 48
-GV = 64
-KS = ((0, 3, "v"), (1, 3, "s"), (2, 4, "v"), (3, 4, "s"), (6, 2, "v"))
+H1 = 48
+SEG = ((6, 0, 4), (7, 4, 6), (2, 6, 8))
+PGW = ((1, 1, 0, 0), (0, 0, 0, 0), (0, 0, 0, 0))
+OFF = ((0,) * 6,) * 3
+PV = ((0, 0, 0, 0), (0, 0, 0, 0), (0, 0, 0, 0))
+WP = 8
+GV = 66
+KV = 9
+KS = ((1, 9, 12), (3, 12, 16))
+KSUM = ((0, 3), (9, 12), (3, 5), (5, 7), (12, 16), (7, 8), (8, 9))
+HSV, SPE = 0, 1
 
-CY, PE, HOP, SAME, REM, FIX = 0.00104, 0.00052, 0.10, 0.06, 6.0, {"v": 0.05, "s": 0.1}
-SCALES = ((1.0, 1.0, 1.0), (0.7, 1.0, 1.2), (1.3, 1.0, 1.0), (1.0, 1.5, 1.2))
-TRIES = 2000
+HOP, SAME, REM, FIX = 0.10, 0.06, 8.0, {"v": 0.055, "s": 0.1}
+TIMES = ((0.0009, 0.0005, 1.45, 3.5, 0, 1.0, 1.0, 0.3), (0.0011, 0.00058, 0.85, 2.3, 0, 1.1, 1.2, 0.2), (0.001, 0.00055, 1.75, 4.8, 0, 1.1, 1.0, 0.15))
+YS = 3
+TIGHT, TRIES, BATCH, SLACK, EPS = 8, 40000, 12, 0.2, 1e-4
 PLAN = []
 
 BF, FP, I32, U16 = "bfloat16", "float32", "int32", "uint16"
@@ -21,28 +31,29 @@ SB = {
     "X0": (W, BF), "X1": (W, BF), "X2": (W, BF), "M1U": (W, BF), "M1L": (W, BF), "M2U": (W, BF), "M2L": (W, BF),
     "C1U": (V, BF), "C1L": (V, BF), "C2U": (V, BF), "C2L": (V, BF), "EK": (128, FP), "KK": (128, BF),
     "YY": (W, BF), "ML": (V, BF), "WT": (V + 128, BF), "AU": (V, BF), "AL": (V, BF),
-    "PU": (PWW, BF), "PL": (PWW, BF), "P2U": (W, BF), "P2L": (W, BF), "P4U": (V, BF), "P4L": (V, BF),
-    "ULI": (200, I32), "ULA": (196, I32), "PP": (392, BF), "LS": (6 * NJ, U16), "THI": (4, I32), "THR": (4, FP),
-    "BI": (4, I32), "BJ": (4, I32), "RLI": (512, I32), "RLW": (648, FP), "SNI": (32, I32), "SNL": (32, U16),
-    "SB0": (480, BF), "SB1": (480, BF),
-    "UW": (16 * 144, BF), "BB": (4 * 144, BF), "II": (256, BF), "NII": (128, BF), "IDF": (128, FP), "ONE": (256, BF),
-    "NONE": (128, BF), "ONF": (128, FP), "OB": (128, BF), "OBT": (128, BF), "NOB": (128, BF), "OB2": (128, BF),
-    "TRI": (128, BF), "EV": (128, BF), "OD": (128, BF), "ZM": (128, BF),
-    "T8": (24, BF), "BI2": (8, BF), "NBI": (8, BF), "ECI": (848, FP), "EC": (848, BF), "JT": (424, BF), "J16": (112, BF),
-    "N1": (128, FP), "N0": (128, BF), "RST": (128, FP), "RS0": (128, FP), "RS2": (1024, BF), "DD": (1024, BF),
-    "DS": (1024, BF), "C24": (24, FP), "DUM": (8, FP), "NW": (8, FP), "T16": (8, FP), "ENI": (8, I32), "ENL": (8, U16),
+    "PT": (2 * W + 128, BF), "P2U": (W, BF), "P2L": (W, BF), "P4U": (V, BF), "P4L": (V, BF),
+    "ULI": (196, I32), "ULA": (196, I32), "PP": (392, BF), "LS": (6 * NJ, U16), "THI": (4, I32), "THR": (4, FP),
+    "THF": (4, FP), "BT": (4, FP), "C15": (8, BF), "JUNK": (424, BF),
+    "RLI": (512, I32), "RLW": (648, FP), "SNI": (32, I32), "SNL": (32, U16),
+    "SB0": (480, BF), "SB1": (480, BF), "SG": (960, BF), "B8": (16, BF), "GS0": (512, BF), "GS1": (512, BF),
+    "UW": (16 * 144, BF), "BB": (3 * 144, BF), "II": (256, BF), "NII": (128, BF), "IDF": (128, FP), "ONE": (256, BF),
+    "OB": (128, BF), "OBT": (128, BF), "NOB": (128, BF), "TRS": (128, BF),
+    "TRI": (128, BF), "EV": (128, BF), "OD": (128, BF), "ZM": (128, BF), "SW": (128, BF),
+    "T8": (48, BF), "ECC": (8, FP), "EC": (848, BF), "JT": (424, BF), "J16": (112, BF),
+    "N1": (128, FP), "N0": (128, BF), "RST": (128, FP), "RS2": (576, BF), "DD": (576, BF),
+    "DS": (576, BF), "C8": (8, BF), "DUM": (8, FP), "NW": (8, FP), "T16": (8, FP), "ENI": (8, I32), "ENL": (8, U16),
     "PI": (4, I32), "PJ": (4, I32), "COL": (8, FP), "GI": (480, FP),
-    "TU": (NJ, FP), "DUS": (NJ, FP), "DH": (NJ, FP), "HL": (NJ, FP), "BAD": (112, BF), "CUM": (112, BF), "UPP": (NJ, FP),
+    "DUS": (NJ, FP), "TU": (NJ, FP), "HB": (NJ, BF), "BAD": (112, BF), "CUM": (112, BF), "UPP": (NJ, FP),
     "TT": (NJ, FP), "HS": (112, BF), "FW": (112, BF), "ZW": (112, FP), "SC": (848, FP), "JL": (8, U16), "HJ": (16, BF),
-    "OH": (128, BF), "QQ": (512, BF), "OJ": (128, BF), "LST": (16, U16), "HV": (16, FP), "CL": (128, U16),
-    "WA": (128, BF), "GG": (W, BF), "AA": (W, BF), "QP": (128, BF), "CAB": (256, BF), "CF": (128, FP), "SM": (128, FP),
-    "ST": (128, BF), "M2": (256, BF), "CP": (128, BF), "VUL": (16, U16), "NB": (8, FP), "HN": (8, FP), "XX": (8, FP),
-    "XY": (8, FP), "RLL": (8, U16), "DVC": (128, FP), "TV": (128, FP), "OU": (NJ, FP), "OL": (NJ, FP),
+    "OH": (128, BF), "QQ": (384, BF), "OJ": (128, BF), "LST": (16, U16), "HV": (16, FP), "CL": (128, U16),
+    "WA": (128, BF), "GG": (W, BF), "AA": (W, BF), "QP": (128, BF), "CAB": (256, BF), "SM": (128, FP),
+    "ST": (128, BF), "M2": (256, BF), "CP": (128, BF), "VUL": (8, U16), "NB": (8, FP),
+    "XY": (8, FP), "RLL": (8, U16), "NV": (256, FP), "K4": (256, BF), "OU": (NJ, FP), "OL": (NJ, FP),
 }
 SCRATCH = {k: ("sbuf", [128, n], d) for k, (n, d) in SB.items()}
 for _b in range(8):
     SCRATCH["ps%d" % _b] = ("psum", [128, 512], FP)
-NDMA = 44
+NDMA = 52
 SEMAPHORES = ["cv", "cs", "cp", "cg", "arr0", "arr1", "snt0", "snt1", "dy0", "dy1", "dy2"] + ["d%d" % _i for _i in range(NDMA)]
 
 
@@ -83,16 +94,16 @@ def rank_program(g, core, T, topo):
     def cost(q, outs, ins, f):
         o, i = outs[0], ins[0] if ins else None
         if q == "p":
-            return max(64, width(o)) * PE * (4 if SB[i[0]][1] == FP else 1)
+            return [max(64, width(o)) * m[1] * (4 if SB[i[0]][1] == FP else 1) for m in TIMES]
         if q == "g":
-            return 0.15 + 2 * width(o) * CY
+            return [0.15 + 2 * width(o) * m[0] for m in TIMES]
         if o[0] == "*":
-            return FIX[q] + width(o) * 3.8 * CY
+            return [FIX[q] + width(o) * m[3] * m[0] for m in TIMES]
         if i is not None and i[0] == "*":
-            return FIX[q] + width(o) * 1.56 * CY
+            return [FIX[q] + width(o) * max(m[2], m[4] if f == 2 else 0) * m[0] for m in TIMES]
         if f is None:
             f = 0.5 if q == "v" and narrow(o, *[x for x in ins if isinstance(x, tuple) and width(x) > 1]) else 1
-        return FIX[q] + max(64, width(o) * f) * CY
+        return [FIX[q] + max(64, width(o) * f) * m[0] for m in TIMES]
 
     def add(q, fn, outs, ins, sem=None, inc=1, free=False, pre=None, f=None, lat=0.0, post=None, after=()):
         rd, wr = [], []
@@ -105,9 +116,9 @@ def rank_program(g, core, T, topo):
                 rd.append(x[2])
             else:
                 wr.append(x)
+        c = [m[7] if inc else 0.5 for m in TIMES] if free else cost(q, outs, ins, f)
         ops.append({"q": q, "fn": fn, "rd": rd, "wr": wr, "sem": sem or "c" + q, "inc": inc, "free": free, "pre": pre, "post": post,
-                    "cost": (0.1 if inc else 1.0) if free else cost(q, outs, ins, f), "lat": lat, "deps": set(after), "order": set(),
-                    "ix": any(isinstance(x, tuple) and x[0] == "*" for x in list(outs) + list(ins))})
+                    "cost": c[0], "costs": c, "lat": lat, "deps": set(after), "order": set()})
         return len(ops) - 1
 
     def cp(o, i):
@@ -127,14 +138,18 @@ def rank_program(g, core, T, topo):
     def mset(o, c):
         return add("v", lambda: g.vector.memset(ap(o), c), [o], [])
 
-    def act(o, i, f=F.Identity, bias=0.0, scale=1.0):
+    def act(o, i, f=F.Identity, bias=0.0, scale=1.0, acc=None):
+        if acc:
+            return add("s", lambda: g.scalar.activation(ap(o), ap(i), f, bias=ap(bias), scale=ap(scale), accum_out=ap(acc)),
+                       [o, acc], [i, bias, scale])
         return add("s", lambda: g.scalar.activation(ap(o), ap(i), f, bias=ap(bias), scale=ap(scale)), [o], [i, bias, scale])
 
     def mms(ms):
         def fn():
             return [g.tensor.matmul(ap(o), ap(l), ap(r), start, stop) for o, l, r, start, stop in ms][-1]
         i = add("p", fn, [m[0] for m in ms], [m[1] for m in ms] + [m[2] for m in ms], lat=0.05)
-        ops[i]["cost"] = sum(cost("p", [m[0]], [m[1]], None) for m in ms)
+        ops[i]["costs"] = [sum(c) for c in zip(*[cost("p", [m[0]], [m[1]], None) for m in ms])]
+        ops[i]["cost"] = ops[i]["costs"][0]
         return i
 
     def mm(o, l, r, start, stop):
@@ -174,15 +189,19 @@ def rank_program(g, core, T, topo):
         return R("UW", 144 * r + 15 - i, 144 * r + 143 - i)
 
     def wrap(out, lhs, src, a, b, first=True, last=True):
-        return mms([(out, lhs(r), R(src, a + r, b, 16), first and r == 0, last and r == 15) for r in range(16)])
+        return [mms([(out, lhs(r), R(src, a + r, b, 16), first and r == 0, last and r == 15) for r in range(r0, r0 + WP)])
+                for r0 in range(0, 16, WP)]
 
     def LS(k, a=0, b=NJ):
         return R("LS", NJ * k + a, NJ * k + b)
 
+    def TRI0(t):
+        return 8 * t * (t + 1)
+
     I_, NI_ = R("II", 0, 128), R("NII")
 
     d0 = dma("y", R("ULI", 0, 98), T.up[:, :])
-    dma("s", R("ULI", 100, 198), T.lo[:, :])
+    dma("s", R("ULI", 98, 196), T.lo[:, :])
     dx = dma("y", R("X0"), T.x[:, :])
     chain([d0, dx, dma("y", R("X1", 0, 16 * H0), T.x[:, 0:16 * H0]), dma("y", R("X1", 16 * H0, V), T.x[:, 16 * H0:V])])
     for b in ("M1U", "M1L", "M2U", "M2L", "YY"):
@@ -191,198 +210,258 @@ def rank_program(g, core, T, topo):
     dma("y", R("THI", 0, 1), T.th[:, :], after=[dx])
     dma("y", R("RLI"), T.rl[:, :], after=[dx])
     dma("y", R("SNI", 0, 30), T.snd[:, :], after=[dx])
-    dma("y", R("X2", 0, V), T.x[:, 0:V], after=[dx])
 
-    fill(R("ONE"), 1)
-    iota(R("PI", 0, 1), [[0, 1]], 0, 1)
-    mset(R("UW"), 0.0)
-    mset(R("BB"), 0.0)
-    sel(R("UW", 15, 2304, 16), R("ONE", 0, 144), [[-1, 16], [-16, 9]], A.is_equal, 0, 1)
-    iota(R("GI"), [[1, 480]], V - 1792)
-    ts(R("PJ", 0, 1), R("PI", 0, 1), 15, A.bitwise_and)
-    ts(R("PJ", 1, 2), R("PI", 0, 1), 1, A.bitwise_and)
-    cp(R("COL", 0, 1), R("PJ", 0, 1))
-    ts(R("COL", 1, 2), R("PJ", 0, 1), 256.0, A.mult)
-    ts(R("COL", 2, 3), R("PJ", 1, 2), -1.0, A.mult, 1.0, A.add)
-    ts(R("COL", 3, 4), R("PJ", 1, 2), 1792.0, A.mult)
-    ts(R("PU", V, W), R("GI"), R("COL", 2, 3), A.mult, R("COL", 3, 4), A.add)
-    cp(R("P2U", V, W), R("PU", V, W))
-    cp(R("P2L", V, W), R("PU", V, W))
-    for m, (lo_, hi_) in ((1, (0, 1)), (2, (2, 3)), (0, (0, 15))):
-        sel(R("T8", 8 * m, 8 * m + 8), R("ONE", 0, 8), [[-16, 8]], A.is_ge, -lo_, 1)
+    def diag(o, c):
+        sel(o, R("ZM"), [[-1, 128]], A.not_equal, 0, 1, c)
+
+    def block(m, lo_, hi_, c):
+        sel(R("T8", 8 * m, 8 * m + 8), R("ZM", 0, 8), [[16, 8]], A.is_gt, lo_, -1, c)
         sel(R("BB", 144 * m + 15, 144 * m + 128, 16), R("T8", 8 * m, 8 * m + 8), [[16, 8]], A.is_ge, hi_, -1)
-    fill(R("NONE"), -1)
-    sel(R("BB", 144 * 3 + 15, 144 * 3 + 128, 16), R("NONE", 0, 8), [[-16, 8]], A.is_equal, -2, 1)
-    sel(R("II"), R("ONE"), [[0, 2], [-1, 128]], A.is_equal, 0, 1)
-    sel(R("NII"), R("NONE"), [[-1, 128]], A.is_equal, 0, 1)
-    iota(R("ECI"), [[4096, 8], [0, NX]], 128)
+
+    chain([mset(R("ONE"), 1.0), mset(R("UW"), 0.0), mset(R("ZM"), 0.0), mset(R("BB"), 0.0)])
+    iota(R("PI", 0, 1), [[0, 1]], 0, 1)
+    iota(R("T16"), [[16, 8]], 0)
     sel(R("OBT"), R("ONE", 0, 128), [[-16, 8], [0, 16]], A.is_ge, 0, 1)
     sel(R("OB"), R("OBT"), [[16, 8], [0, 16]], A.is_ge, 15, -1)
-    sel(R("OBT"), R("OB"), [[1, 128]], A.is_gt, 0, -1)
-    sel(R("TRI"), R("OB"), [[1, 128]], A.is_ge, 0, -1)
-    tt(R("TRI"), R("TRI"), R("OBT"), A.add)
-    fill(R("BAD", NJ, 112), 1)
-    fill(R("CUM", 0, 1), 0)
-    fill(R("HS", NJ, 112), 256)
-    fill(R("FW", NJ, 112), FAR // 2)
-    fill(R("HJ", 0, 8), 256)
-    iota(R("JT"), [[0, 4], [1, NX]], 0)
-    iota(R("N1"), [[2, 128]], 1)
-    fill(R("ZM"), 0)
-    fill(R("WT", V, V + 128), 0)
-    fill(R("RLW", 512, 648), 0)
-    iota(R("T16"), [[16, 8]], 0)
-    iota(R("ENI"), [[16, 8]], 15)
-    iota(R("J16"), [[16, 112]], 0)
-    iota(R("N0"), [[1, 128]], 0)
-    fill(R("RS0"), -BIG)
-    sel(R("RST"), R("RS0"), [[0, 8], [1, 16]], A.not_equal, 0, 0, float(BIG))
-    iota(R("KK"), [[0, 8], [1, 16]], 0)
-    sel(R("EV"), R("OB"), [[0, 64], [1, 2]], A.is_equal, 0, 0)
-    sel(R("OD"), R("OB"), [[0, 64], [1, 2]], A.not_equal, 0, 0)
-    fill(R("ONF"), 1)
-    sel(R("IDF"), R("ONF"), [[-1, 128]], A.is_equal, 0, 1)
-    fill(R("C24", 8, 16), 0)
-    fill(R("C24", 16, 24), FAR)
-    fill(R("DD"), BIG)
-    fill(R("RS2"), 0)
-    fill(R("RS2", 0, 1024, 128), BIG)
+    sel(R("II"), R("ONE"), [[0, 2], [-1, 128]], A.is_equal, 0, 1)
+    sel(R("UW", 15, 2304, 16), R("ONE", 0, 144), [[-1, 16], [-16, 9]], A.is_equal, 0, 1)
+    iota(R("GI"), [[1, 480]], V - 1792)
+    for z, c in ((R("BAD", NJ, 112), 1), (R("CUM", 0, 1), 0), (R("HS", NJ, 112), 256), (R("HJ", 0, 8), 256), (R("FW", NJ, 112), SPARE)):
+        fill(z, c)
+    iota(R("C15", 0, 2), [[15, 2]], -15)
+    block(1, 0, 1, 1.0)
+    block(2, 2, 3, 1.0)
+    diag(R("NII"), -1.0)
+    ts(R("PJ", 0, 1), R("PI", 0, 1), 15, A.bitwise_and)
+    ts(R("PJ", 1, 2), R("PI", 0, 1), 1, A.bitwise_and)
+    cp(R("COL", 0, 2), R("PJ", 0, 2))
+    act(R("COL", 2, 3), R("COL", 1, 2), bias=1.0, scale=-1.0)
+    act(R("COL", 3, 4), R("COL", 1, 2), F.Copy, scale=1792.0)
+    ts(R("COL", 4, 5), R("PJ", 0, 1), 8.0, A.is_ge)
+    act(R("COL", 5, 6), R("COL", 4, 5), bias=1.0, scale=-1.0)
+    act(R("PT", V, W), R("GI"), bias=R("COL", 3, 4), scale=R("COL", 2, 3))
+    dma("y", R("P2U", V, W), R("PT", V, W))
+    dma("y", R("P2L", V, W), R("PT", V, W))
     cp(R("THR", 0, 1), R("THI", 0, 1))
     cp(R("RLW", 0, 512), R("RLI"))
     cp(R("SNL", 0, 30), R("SNI", 0, 30))
-    cp(R("ENL"), R("ENI"))
-    act(R("EC"), R("ECI"), bias=R("COL", 1, 2))
+    act(R("THF", 0, 1), R("THR", 0, 1), F.Copy)
     act(R("NOB"), R("OB"), F.Copy, scale=-256.0)
-    act(R("OB2"), R("OB"), F.Copy, scale=256.0)
-    act(R("BI2"), R("OB", 0, 128, 16), F.Copy, scale=32.0)
-    act(R("NBI"), R("OB", 0, 128, 16), F.Copy, scale=-16.0)
-    act(R("NW"), R("T16"), bias=R("COL", 0, 1))
-    act(R("C24", 0, 8), R("NW"), F.Copy, scale=1024.0)
-    act(R("DUM"), R("NW"), bias=513.0)
+    act(R("B8", 0, 8), R("OB", 0, 128, 16), F.Copy, scale=256.0)
+    act(R("B8", 8, 16), R("OB", 0, 128, 16), F.Copy, scale=-512.0)
 
-    cp(LS(0), R("ULI", 0, 98))
-    cp(LS(1), R("ULI", 100, 198))
-    for t in range(2):
-        ts(R("ULA", 98 * t, 98 * t + 98), R("ULI", 100 * t, 100 * t + 98), 511, A.bitwise_and)
+    def late():
+        block(0, 0, 15, 1.0)
+        sel(R("TRS"), R("OB"), [[1, 128]], A.is_gt, 0, -1)
+        sel(R("TRI"), R("OB"), [[1, 128]], A.is_ge, 0, -1)
+        iota(R("JT"), [[0, 4], [2, NX]], -NX)
+        diag(R("IDF"), 1.0)
+        iota(R("N1"), [[2, 128]], 1)
+        fill(R("RLW", 512, 648), 0)
+        fill(R("WT", V, V + 128), 0)
+        iota(R("KK"), [[0, 8], [-1, 16]], 0)
+        sel(R("SW"), R("NOB"), [[0, 8], [1, 16]], A.is_ge, -KV, 0)
+        iota(R("ENI"), [[16, 8]], 15)
+        cp(R("ENL"), R("ENI"))
+        iota(R("J16"), [[16, 112]], 0)
+        iota(R("N0"), [[1, 128]], 0)
+        fill(R("RST"), 4 * BIG)
+        fill(R("RST", 0, 128, 16), -4 * BIG)
+        sel(R("EV"), R("OB"), [[0, 64], [1, 2]], A.is_equal, 0, 0)
+        sel(R("OD"), R("OB"), [[0, 64], [1, 2]], A.not_equal, 0, 0)
+        fill(R("RS2"), 0)
+        for t in range(8):
+            fill(R("RS2", TRI0(t), TRI0(t) + 1), BIG)
+        fill(R("PT", 2 * W, 2 * W + 128), 0)
+        diag(R("K4", 0, 128), 4096.0)
+        diag(R("K4", 128, 256), -4096.0)
+
+    act(R("NW"), R("T16"), bias=R("COL", 0, 1))
+    act(R("C8"), R("NW"), F.Copy, scale=1024.0)
+    act(R("DUM"), R("NW"), bias=513.0)
+    act(R("ECC"), R("NW"), bias=128.0, scale=256.0)
+    for t in range(SEG[2][1]):
+        act(R("EC", NX * t, NX * (t + 1)), R("ZM", 0, NX), bias=R("ECC", t, t + 1))
+
+    ts(R("ULA"), R("ULI"), 511, A.bitwise_and)
     ts(R("PP", 0, 196), R("ULA"), -256.0, A.add)
-    for t in range(2):
-        tt(R("PP", 196 + 98 * t, 294 + 98 * t), R("ULI", 100 * t, 100 * t + 98), R("PP", 98 * t, 98 * t + 98), A.subtract)
-    ids = []
-    for r in range(16):
-        parts = ((0, 0), (2, 98), (1, 196), (3, 294))
-        ids.append(mms([(PS(r % 8, 0, NJ), UWs(r, i), R("PP", a, a + NJ), i == 0, i == 3) for i, a in parts]))
-        act(R("PU", r, V, 16), PS(r % 8, 0, NJ), F.Copy)
-    chain(ids)
-    dma("y", R("PL", 0, W), R("PU", 0, W))
+    tt(R("PP", 196, 392), R("ULI"), R("PP", 0, 196), A.subtract)
+    cp(R("LS", 0, 2 * NJ), R("ULI"))
+    for r in range(8):
+        for h in range(2):
+            for parts in (((0, 0), (2, 98)), ((1, 196), (3, 294))):
+                mms([(PS(r, h, 2 * NJ, 2), UWs(r + 8 * h, i), R("PP", a, a + NJ), i == 0, i == 3) for i, a in parts])
+        act(R("PT", r, V, 8), PS(r, 0, 2 * NJ), F.Copy)
 
     for rnd in range(RO):
         X, XO = "X%d" % rnd, "X%d" % ((rnd + 1) % RO)
-        PLw = "PU" if rnd == 0 else "PL"
+        L0 = 0 if rnd == 0 else W
         last = rnd == RO - 1
-        steps, pgs = [], []
+        steps, pgs, diffs, vs, lists = [], [], [], [], {}
+
+        def ahead(k):
+            if k in lists and rnd:
+                ops[steps[-1]]["order"].add(lists[k])
 
         def step(o, win, own, k, a, b):
             steps.append(tt(R(o, 16 * a, 16 * b), IX(R(win), LS(k, a, b)), R(own, 16 * a, 16 * b), A.max))
             if rnd and win == X:
                 ops[-1]["pre"] = ("arr%d" % (rnd - 1), 16)
 
-        def step2(o, win, own, k, twin, halves):
-            for h, (a, b) in enumerate(halves):
-                step(o, win, own, k, a, b)
-                if h == 0:
-                    dma("y", R(twin, 16 * a, 16 * b), R(o, 16 * a, 16 * b))
+        def shared(o, win, k, a, b, c):
+            if a < b:
+                gb = "GS%d" % (k % 2)
+                act(R(gb, 0, 16 * (b - a)), IX(R(win), LS(k, a, b)), F.Copy)
+                if rnd and win == X:
+                    ops[-1]["pre"] = ("arr%d" % (rnd - 1), 16)
+                mm(PS(c, 0, 16 * (b - a)), I_, R(win, 16 * a, 16 * b), True, True)
+                steps.append(tt(R(o, 16 * a, 16 * b), PS(c, 0, 16 * (b - a)), R(gb, 0, 16 * (b - a)), A.max))
+
+        def step2(o, win, own, k, twin, halves, c):
+            e, e2 = NJ - OFF[rnd][k], NJ - OFF[rnd][k + 2]
+            for h, (a, b) in enumerate(halves + ((e, NJ),)):
+                if h < len(halves):
+                    b = min(b, e)
+                    step(o, win, own, k, a, b)
                 else:
+                    shared(o, win, k, a, b, c)
+                b = min(b, e2)
+                if h < len(halves) - 1:
+                    dma("y", R(twin, 16 * a, 16 * b), R(o, 16 * a, 16 * b))
+                elif a < b:
                     sel(R(twin, 16 * a, 16 * b), R(o, 16 * a, 16 * b), [[0, 16 * (b - a)]], A.is_ge, 0, 0)
 
-        def pg(o, win, k):
-            pgs.append(act(R(o, 0, V), IX(R(win, 0, W), LS(k)), F.Copy))
+        def pg(o, win, k, w0, parts, m, banks):
+            for (a, b), c in zip(parts, banks):
+                e = min(b, NJ - PV[rnd][k])
+                pgs.append(act(R(o, 16 * a, 16 * e), IX(R(win, w0, w0 + W), LS(k, a, e)), F.Copy))
+                if e < b:
+                    cp(R(o, 16 * e, 16 * b), IX(R(win, w0, w0 + W), LS(k, e, b)))
+                if PGW[rnd][k]:
+                    wrap(PS(c, a, b), lambda r: BR(m, r), o, 16 * a, 16 * b)
+                    cp(LS(k + 2, a, b), PS(c, a, b))
+            if not PGW[rnd][k]:
+                wrap(PS(banks[0], 0, NJ), lambda r: BR(m, r), o, 0, V)
+                lists[k] = cp(LS(k + 2), PS(banks[0], 0, NJ))
 
-        def far(buf, out, c):
-            a, b = CH[c]
-            mm(PS(c, 0, 16 * (b - a)), I_, R(buf, 16 * a, 16 * b), False, True)
-            act(R(out, 16 * a, 16 * b), PS(c, 0, 16 * (b - a)), F.Abs)
+        def far(buf, out, a, b, c, scale=1.0):
+            diffs.append(mm(PS(c, 0, 16 * (b - a)), I_, R(buf, 16 * a, 16 * b), False, True))
+            pgs.append(act(R(out, 16 * a, 16 * b), PS(c, 0, 16 * (b - a)), F.Abs, scale=scale))
 
-        def negw(c):
-            a, b = CH[c]
+        def negw(a, b, c):
             mm(PS(c, 0, 16 * (b - a)), NI_, R("WT", 16 * a, 16 * b), True, False)
 
         up_, dn_ = ((0, H0), (H0, NJ)), ((H0, NJ), (0, H0))
-        step2("M1U", X, XO, 0, "C1U", up_)
-        pg("P2U", "PU", 0)
-        step2("M1L", X, XO, 1, "C1L", up_)
-        pg("P2L", PLw, 1)
-        wrap(PS(6, 0, NJ), lambda r: UWs(0, r), "PU", 0, V, True, False)
-        wrap(PS(6, 0, NJ), lambda r: BR(3, r), PLw, 0, V, False, True)
-        wrap(PS(7, 0, NJ), lambda r: UWs(2, r), PLw, 0, V)
-        wrap(PS(4, 0, NJ), lambda r: BR(1, r), "P2U", 0, V)
-        cp(LS(2), PS(4, 0, NJ))
-        step2("M2U", "M1U", "C1U", 2, "C2U", dn_)
-        wrap(PS(5, 0, NJ), lambda r: BR(2, r), "P2L", 0, V)
-        pg("P4U", "P2U", 2)
-        cp(LS(3), PS(5, 0, NJ))
-        step2("M2L", "M1L", "C1L", 3, "C2L", dn_)
-        pg("P4L", "P2L", 3)
-        wrap(PS(4, 0, NJ), lambda r: BR(1, r), "P4U", 0, V)
-        cp(LS(4), PS(4, 0, NJ))
-        wrap(PS(5, 0, NJ), lambda r: BR(2, r), "P4L", 0, V)
-        cp(LS(5), PS(5, 0, NJ))
-        act(R("DH"), PS(6, 0, NJ), F.Copy)
-        act(R("HL"), PS(7, 0, NJ), F.Copy)
-        for h in range(2):
-            mm(PS(6 + h, 0, 424), I_, R("EC", 424 * h, 424 * h + 424), True, False)
-        for c, (a, b) in enumerate(CH):
-            negw(c)
-            step("YY", "M2U", "C2U", 4, a, b)
-            far("YY", "AU", c)
-        wrap(PS(4, 0, JA), lambda r: BR(0, r), "AU", 0, 16 * JA)
-        wrap(PS(4, JA, NJ), lambda r: BR(0, r), "AU", 16 * JA, V)
-        act(R("TU"), PS(4, 0, NJ), bias=R("THR", 0, 1), scale=-1.0)
-        act(R("DUS"), PS(4, 0, NJ), F.Copy)
-        for c, (a, b) in enumerate(CH):
-            negw(c)
+        step2("M1U", X, XO, 0, "C1U", ((0, H1), (H1, NJ)) if rnd else up_, 1)
+        whole = ((0, NJ),)
+        pg("P2U", "PT", 0, 0, dn_ if PGW[rnd][0] else ((0, H1), (H1, NJ)), 1, (0, 1))
+        step2("M1L", X, XO, 1, "C1L", up_, 3)
+        ahead(0)
+        pg("P2L", "PT", 1, L0, dn_ if PGW[rnd][1] else whole, 2, (2, 3))
+        DH, HL = PS(5, 128, 128 + NJ), PS(4, 128, 128 + NJ)
+        wrap(HL, lambda r: UWs(2, r), "PT", L0, L0 + V)
+        act(R("HB"), HL, F.Copy)
+        wrap(DH, lambda r: UWs(0, r), "PT", 0, V, True, False)
+        mm(DH, NI_, R("HB"), False, True)
+        d3_ = ((H0, NJ), (NJ - H0, H0), (0, NJ - H0)) if 2 * H0 > NJ else dn_
+        step2("M2U", "M1U", "C1U", 2, "C2U", d3_, 4)
+        ahead(1)
+        pg("P4U", "P2U", 2, 0, up_ if PGW[rnd][2] else whole, 1, (1, 3))
+        step2("M2L", "M1L", "C1L", 3, "C2L", d3_, 7)
+        ahead(2)
+        pg("P4L", "P2L", 3, 0, up_ if PGW[rnd][3] else whole, 2, (4, 5))
+        if rnd == 0:
+            late()
+            twin = max(i for i, o in enumerate(ops) if o["q"] == "y")
+            dma("y", R("X2", 0, V), T.x[:, 0:V], after=[twin])
+            dma("y", R("PT", W, 2 * W), R("PT", 0, W), after=[twin])
+        else:
+            nb = R("CUM", NJ, NJ + 1)
+            mms([(PS(2, 256, 258), I_, R("C15", 0, 2), True, False), (PS(2, 256, 257), R("ONE", 0, 128), nb, False, False),
+                 (PS(2, 256, 257), R("ONE", 0, 128), nb, False, False), (PS(2, 257, 258), R("ONE", 0, 128), nb, False, False),
+                 (PS(2, 257, 258), R("IDF"), R("THF", 0, 1), False, True)])
+            pgs.append(act(R("BT", 0, 1), PS(2, 256, 257), bias=12582912.0, scale=1.0 / 32))
+            pgs.append(act(R("BT", 1, 2), R("BT", 0, 1), bias=201326592.0, scale=-16.0))
+            pgs.append(act(R("THR", 0, 1), PS(2, 257, 258), bias=R("BT", 1, 2)))
+        for a, b, c in CU:
+            negw(a, b, c)
+            if a < NJ - OFF[rnd][4]:
+                step("YY", "M2U", "C2U", 4, a, b)
+            else:
+                shared("YY", "M2U", 4, a, b, 7)
+            far("YY", "AU", a, b, c)
+        ahead(3)
+        if not last:
+            pgs.append(act(R("SG", 0, 480), IX(R("YY", 0, V), R("SNL", 0, 30)), F.Copy, scale=R("COL", 5, 6)))
+        for k, (a, b, c) in enumerate(CW):
+            negw(a, b, c)
             step("ML", "M2L", "C2L", 5, a, b)
-            far("ML", "AL", c)
+            far("ML", "AL", a, b, c)
+            if k == 0:
+                wrap(PS(4, 0, JU), lambda r: BR(0, r), "AU", 0, 16 * JU)
+                wrap(PS(4, JU, NJ), lambda r: BR(0, r), "AU", 16 * JU, V)
+        ts(R("TU"), PS(4, 0, NJ), -1.0, A.mult, R("THR", 0, 1), A.add)
+        act(R("DUS"), PS(4, 0, NJ), F.Copy)
         wrap(PS(5, 0, JA), lambda r: BR(0, r), "AL", 0, 16 * JA)
-        wrap(PS(0, JA, NJ), lambda r: BR(0, r), "AL", 16 * JA, V)
+        wrap(PS(5, JA, NJ), lambda r: BR(0, r), "AL", 16 * JA, V)
+        for c, a, b in SEG[:2]:
+            mm(PS(c, 0, NX * (b - a)), I_, R("EC", NX * a, NX * b), True, False)
         chain(steps)
         chain(pgs)
-        for k in range(8):
-            dma("y", R("YY", 0, V, 1, 16 * k + 8, 16 * k + 16), R("ML", 0, V, 1, 16 * k + 8, 16 * k + 16), s="dy%d" % rnd)
+        chain(diffs)
+        for p in range(8, 128, 16):
+            dma("s" if p < 16 * YS else "y", R("YY", 0, V, 1, p, p + 8), R("ML", 0, V, 1, p, p + 8), s="dy%d" % rnd)
         if last:
             dma("y", T.y[:, :], R("YY", 0, V))
-        for a, b, dl in ((0, JA, PS(5, 0, JA)), (JA, NJ, PS(0, JA, NJ))):
-            tt(R("BAD", a, b), dl, R("TU", a, b), A.is_gt)
-            tt(R("UPP", a, b), dl, R("DUS", a, b), A.is_le)
-            tt(R("TT", a, b), R("UPP", a, b), R("DH", a, b), A.mult)
-            tt(R("HS", a, b), R("TT", a, b), R("HL", a, b), A.add)
-        scan(R("CUM", 1, NX + 1), R("BAD", 0, NX), R("BAD", 0, NX), 0.0, A.add, A.max)
-        chain([mms([(PS(6 + h, NX * t, NX * (t + 1)), R("NOB"), R("CUM", 1, NX + 1), False, t == 3) for t in range(4)]) for h in range(2)])
-        mms([(PS(1, 0, NX), R("OB"), R("CUM", 0, NX), True, False), (PS(1, 0, NX), R("OB"), R("CUM", 0, NX), False, False),
-             (PS(1, 0, NX), R("TRI"), R("BAD", 0, NX), False, True)])
-        act(R("ZW", 0, NX), PS(1, 0, NX), F.Copy)
-        for h in range(2):
-            scan(R("SC", 424 * h, 424 * h + 424), R("JT"), PS(6 + h, 0, 424), 1000.0, A.min, A.max)
-        cp(R("JL"), R("SC", NX - 1, 848, NX))
-        act(R("HJ", 8, 16), R("SC", NX - 1, 848, NX), F.Copy, scale=16.0)
-        for c, nk, q in KS:
-            mm(PS(c, 0, 128 * nk), R("ZM"), R("WT", 0, 128 * nk), True, False)
+        else:
+            ts(R("SG", 480, 960), IX(R("ML"), R("SNL", 0, 30)), R("COL", 4, 5), A.mult)
+            if SPE:
+                mm(PS(3, 0, 480), I_, R("SG", 0, 480), True, SPE == 1)
+            if SPE == 2:
+                mm(PS(3, 0, 480), I_, R("SG", 480, 960), False, True)
+            for a, b in ((0, 2 * NG), (2 * NG, 3 * NG)):
+                if SPE == 2:
+                    act(R("SB%d" % rnd, a, b), PS(3, a, b), F.Copy)
+                    continue
+                vs.append(tt(R("SB%d" % rnd, a, b), PS(3, a, b) if SPE else R("SG", a, b), R("SG", 480 + a, 480 + b), A.add))
+        vs.append(tt(R("BAD", 0, NJ), PS(5, 0, NJ), R("TU"), A.is_gt))
+        vs += [scan(R("CUM", 1, NX + 1), R("BAD", 0, NX), R("BAD", 0, NX), 0.0, A.add, A.max),
+              tt(R("UPP"), PS(5, 0, NJ), R("DUS"), A.is_le), tt(R("TT"), DH, R("UPP"), A.mult)]
+        if HSV:
+            tt(R("HS", 0, NJ), HL, R("TT"), A.add)
+        else:
+            mms([(PS(1, 0, NJ), I_, R("HB"), True, False), (PS(1, 0, NJ), R("IDF"), R("TT"), False, True)])
+            act(R("HS", 0, NJ), PS(1, 0, NJ), F.Copy)
+        for c, a, b in SEG[:2]:
+            mms([(PS(c, NX * t, NX * (t + 1)), R("NOB"), R("CUM", 1, NX + 1), False, t == b - a - 1) for t in range(b - a)])
+        mm(PS(SEG[2][0], 0, NX), R("NOB"), R("CUM", 1, NX + 1), True, True)
+        mms([(PS(0, 0, NX), R("TRI"), R("BAD", 0, NX), True, False), (PS(0, 0, NX), R("TRS"), R("BAD", 0, NX), False, False)])
+        mms([(PS(0, 0, NX), R("OB"), R("CUM", 0, NX), False, False), (PS(0, 0, NX), R("OB"), R("CUM", 0, NX), False, True)])
+        chain(vs + [scan(R("SC", NX * a, NX * b), R("JT", 0, NX * (b - a)), PS(c, 0, NX * (b - a)), 1000.0, A.min, A.max)
+                    for c, a, b in SEG[:2]])
+        c, a, b = SEG[2]
+        for t in range(a, b):
+            act(R("JUNK", NX * (t - a), NX * (t - a + 1)), PS(c, 0, NX), F.Sign, bias=R("ECC", t, t + 1), acc=R("SC", NX * t + NX - 1, NX * t + NX))
+        act(R("ZW", 0, NX), PS(0, 0, NX), F.Copy)
+        ts(R("JL"), R("SC", NX - 1, 848, NX), 0.5, A.mult, NX / 2, A.add)
+        act(R("HJ", 8, 16), R("SC", NX - 1, 848, NX), bias=8.0 * NX, scale=8.0)
+        for c, k0, k1 in KS:
+            mm(PS(c, 0, 128 * (k1 - k0)), R("ZM"), R("WT", 0, 128 * (k1 - k0)), True, False)
         mm(PS(4, 256, 384), I_, R("KK"), True, False)
         tt(R("OH"), IX(R("ZW", 0, NX), R("JL")), R("N1"), A.is_equal)
         act(R("QQ", 128, 256), R("OH"), F.Copy, scale=R("COL", 0, 1))
         tt(R("QQ", 0, 128), IX(R("HS", 0, NX), R("JL")), R("OH"), A.mult)
         mm(PS(5, 128, 144), I_, R("HJ"), True, False)
         wrap(PS(5, 128, 144), lambda r: BR(0, r), "QQ", 0, 256, False, True)
-        act(R("FW", 0, NJ), R("UPP"), bias=float(FAR), scale=-float(FAR))
-        tt(R("OJ"), IX(R("J16", 0, NX), R("JL")), R("OH"), A.mult)
+        act(R("FW", 0, NJ), R("UPP"), bias=float(W), scale=-float(W))
+        act(R("OJ"), IX(R("J16", 0, NX), R("JL")), F.Copy)
         tt(R("QQ", 256, 384), IX(R("FW", 0, NX), R("JL")), R("OH"), A.mult)
         cp(R("LST"), PS(5, 128, 144))
         hl, vl = R("LST", 0, 8), R("LST", 8, 16)
         if not last:
-            act(R("SB%d" % rnd), IX(R("YY"), R("SNL", 0, 30)), F.Copy)
-
-            def send(rnd=rnd):
+            def send(rnd, ds):
                 tr = []
-                for d in (1, 2, 3):
+                for d in ds:
                     dst = cores[(rank + d) % n]
                     rid, pid = topo.addr(dst, core)
                     e = topo.engines(core, dst)
@@ -391,10 +470,12 @@ def rank_program(g, core, T, topo):
                     tr.append(RemoteDMATransfer(
                         dst_ids=[DstId(rid=rid, pnc=pid)], dma_engine_mask=sum(1 << x for x in e), remote_sem=T.sem["arr%d" % rnd],
                         src=ap(R("SB%d" % rnd, NG * (d - 1), NG * d)), dst=ap(R("X%d" % (rnd + 1), V + NG * (d - 1), V + NG * d))))
-                g.remote_dma_fused(tr[:2], local_sem=T.sem["snt%d" % rnd])
-                g.remote_dma_fused(tr[2:], local_sem=T.sem["snt%d" % rnd])
-                return None
-            add("g", send, [], [R("SB%d" % rnd)], free=True, inc=0, lat=REM, post="arr%d" % rnd)
+                g.remote_dma_fused(tr, local_sem=T.sem["snt%d" % rnd])
+            ids = []
+            for ds in ((1, 2), (3,)):
+                z = R("SB%d" % rnd, NG * (ds[0] - 1), NG * ds[-1])
+                ids.append(add("g", lambda rnd=rnd, ds=ds: send(rnd, ds), [], [z], free=True, inc=0, lat=REM, post="arr%d" % rnd))
+            chain(ids)
         cp(R("CL"), IX(R("RLW"), hl))
         act(R("WA"), IX(R("WT"), vl), F.Copy)
         cp(R("GG", 0, 16 * GV), IX(R("YY"), R("CL", 0, GV)))
@@ -402,70 +483,64 @@ def rank_program(g, core, T, topo):
         if not last:
             for b in ("M1U", "M1L", "M2U", "M2L", "YY"):
                 dma("y", R(b, V, W), R("X%d" % (rnd + 1), V, W), pre=("arr%d" % rnd, 16))
-        ids, k0 = [], 0
-        for c, nk, q in KS:
-            mms([(PS(c, 128 * k, 128 * k + 128), NI_, R("WA"), False, False) for k in range(nk)])
-            ids.append(mms([(PS(c, 128 * k, 128 * k + 128), I_, R("GG", k0 + k, W, 16), False, k == nk - 1) for k in range(nk)]))
-            k0 += nk
-        ids.append(mms([(PS(4, 256 + k, 384, 16), R("GG", k, W, 16), R("NBI"), False, False) for k in range(16)]))
+        ids = []
+        mm(PS(0, 0, 128), I_, R("WA"), True, True)
+        for c, k0, k1 in KS:
+            mms([(PS(c, 128 * (k - k0), 128 * (k - k0 + 1)), I_, R("WA"), False, False) for k in range(k0, k1)])
+            ids.append(mms([(PS(c, 128 * (k - k0), 128 * (k - k0 + 1)), NI_, R("GG", k, W, 16), False, k == k1 - 1) for k in range(k0, k1)]))
+        mm(PS(4, 256, 384), R("WA"), R("SW"), False, False)
+        ids.append(mms([(PS(4, 256 + k, 384, 16), R("GG", k, W, 16), R("B8", 0, 8), False, False) for k in range(KV)]))
         chain(ids)
         act(R("QP"), IX(R("RLW"), hl), bias=191.5009765625, scale=1.0 / 512)
-        k0 = 0
-        for c, nk, q in KS:
-            if q == "s":
-                act(R("AA", 128 * k0, 128 * (k0 + nk)), PS(c, 0, 128 * nk), F.Relu)
-            else:
-                ts(R("AA", 128 * k0, 128 * (k0 + nk)), PS(c, 0, 128 * nk), 0.0, A.max)
-            mms([(PS(4, 256 + k, 384, 16), R("AA", 128 * k, 128 * k + 128), R("BI2"), False, k == 15) for k in range(k0, k0 + nk)])
-            k0 += nk
+        chain([tt(R("AA", 128 * k, 128 * k + 128), PS(0, 0, 128), R("GG", k, W, 16), A.max) for k in range(KV)])
+        for c, k0, k1 in KS:
+            act(R("AA", 128 * k0, 128 * k1), PS(c, 0, 128 * (k1 - k0)), F.Abs)
+        for k0, k1 in KSUM:
+            mms([(PS(4, 256 + k, 384, 16), R("AA", 128 * k, 128 * k + 128), R("B8", 8, 16) if k < KV else R("NOB", 0, 128, 16), False,
+                  k == KSUM[-1][1] - 1) for k in range(k0, k1)])
         act(R("CAB", 128, 256), R("QP"), bias=-98048.0, scale=512.0)
         act(R("HV"), PS(5, 128, 144), F.Copy)
-        act(R("QQ", 384, 512), R("QQ", 256, 384), F.Copy, scale=-1.0)
-        scan(R("SM"), R("RST"), PS(4, 256, 384), 0.0, A.max, A.min)
+        scan(R("SM"), R("RST"), PS(4, 256, 384), 0.0, A.min, A.max)
         cp(R("EK"), PS(4, 256, 384))
-        tt(R("ST"), IX(R("SM"), R("ENL")), R("EK"), A.is_equal)
-        mms([(PS(7, 0, 24), R("IDF"), R("C24"), True, False), (PS(7, 0, 16), R("IDF"), R("HV"), False, False),
-             (PS(7, 16, 24), R("IDF"), R("HV", 8, 16), False, False)])
-        mms([(PS(5, 256, 384), I_, R("N0"), True, False), (PS(5, 256, 384), R("OB2"), R("QQ", 0, 128), False, True)])
+        st = tt(R("ST"), IX(R("SM"), R("ENL")), R("EK"), A.is_equal)
+        mms([(PS(5, 256, 384), NI_, R("N0"), True, False), (PS(5, 256, 384), R("NOB"), R("QQ", 0, 128), False, True)])
         mm(PS(0, 0, 256), R("ST"), R("II"), True, True)
-        wrap(PS(7, 8, 24), lambda r: BR(0, r), "QQ", 256, 512, False, True)
-        tt(R("CAB", 0, 128), IX(R("RLW"), hl), R("CAB", 128, 256), A.subtract)
-        act(R("NB"), R("HV", 0, 8), bias=67108864.0, scale=-262144.0)
-        act(R("CF"), IX(R("RLW"), hl), F.Copy)
+        mm(PS(7, 8, 16), R("IDF"), R("HV", 8, 16), True, False)
+        wrap(PS(7, 8, 16), lambda r: BR(0, r), "QQ", 256, 384, False, True)
+        chain([st, tt(R("CAB", 0, 128), IX(R("RLW"), hl), R("CAB", 128, 256), A.subtract)])
+        act(R("NB"), R("HV", 0, 8), bias=-67108864.0, scale=262144.0)
         tt(R("M2"), PS(0, 0, 256), R("CAB"), A.mult)
         mms([(PS(1, 0, 128), R("EV"), R("M2", 0, 128), True, False), (PS(1, 0, 128), R("OD"), R("M2", 128, 256), False, True)])
-        mms([(PS(2, 0, 128), R("OB"), R("OJ"), True, False), (PS(2, 0, 128), R("OB"), R("QQ", 128, 256), False, False),
-             (PS(2, 0, 128), NI_, R("CAB", 0, 128), False, False), (PS(2, 0, 128), NI_, R("CAB", 128, 256), False, True)])
-        cp(R("VUL"), PS(7, 8, 24))
-        act(R("HN"), PS(7, 0, 8), F.Copy)
-        cp(R("CP"), PS(1, 0, 128))
-        act(R("DVC"), PS(2, 0, 128), F.Copy)
+        mms([(PS(2, 0, 256), R("ST"), R("K4"), True, False), (PS(2, 0, 128), I_, R("OJ"), False, False),
+             (PS(2, 0, 128), R("OB"), R("QQ", 128, 256), False, False), (PS(2, 0, 128), R("NOB"), R("ONE", 0, 128), False, False),
+             (PS(2, 128, 256), I_, R("CAB", 0, 128), False, False), (PS(2, 128, 256), I_, R("CAB", 128, 256), False, True)])
+        cp(R("VUL"), PS(7, 8, 16))
         for t in range(8):
-            w_ = 16 * (t + 1)
-            act(R("DD", 128 * t, 128 * t + w_), PS(5, 256, 256 + w_), F.Abs, bias=R("NB", t, t + 1), scale=1024.0)
-        cp(IX(R("PU"), R("VUL", 0, 8)), R("CP"))
-        wrap(PS(4, 0, NJ), lambda r: BR(1, r), "PU", 0, V)
-        cp(IX(R("PL"), R("VUL", 8, 16)), R("CP"))
-        wrap(PS(5, 0, NJ), lambda r: BR(2, r), "PL", 0, V)
-        tt(R("TV"), PS(0, 0, 128), R("DVC"), A.mult)
-        scan(R("DS"), R("RS2"), R("DD"), 0.0, A.max, A.min)
-        tt(R("XX"), R("HN"), R("DS", 127, 1024, 128), A.subtract)
-        tt(R("XY"), R("XX"), R("DUM"), A.min)
-        cp(R("RLL"), R("XY"))
-        tt(IX(R("RLW"), R("RLL")), R("TV"), R("CF"), A.add)
+            act(R("DD", TRI0(t), TRI0(t + 1)), PS(5, 256, 256 + 16 * (t + 1)), F.Abs, bias=R("NB", t, t + 1), scale=1024.0)
+        act(R("NV"), PS(2, 0, 256), F.Copy)
+        ids = [scan(R("DS"), R("RS2"), R("DD"), 0.0, A.max, A.min), cp(R("CP"), PS(1, 0, 128))]
+        ids.append(cp(IX(R("PT"), R("VUL")), R("CP")))
+        mms([(PS(3, 0, 8), I_, R("C8"), True, False), (PS(3, 0, 8), R("IDF"), R("HV", 0, 8), False, False)])
+        mms([(PS(3, t, t + 1), NI_, R("DS", TRI0(t + 1) - 1, TRI0(t + 1)), False, t == 7) for t in range(8)])
+        if last:
+            ws = wrap(PS(4, 0, NJ), lambda r: BR(1, r), "PT", 0, V)
+        else:
+            ws = wrap(PS(4, 0, H1), lambda r: BR(1, r), "PT", 0, 16 * H1) + wrap(PS(6, H1, NJ), lambda r: BR(1, r), "PT", 16 * H1, V)
+        chain(ws + wrap(PS(5, 0, NJ), lambda r: BR(2, r), "PT", W, W + V))
+        ids += [tt(R("XY"), PS(3, 0, 8), R("DUM"), A.min), cp(R("RLL"), R("XY"))]
+        tt(IX(R("RLW"), R("RLL")), R("NV", 0, 128), R("NV", 128, 256), A.max)
         if not last:
-            mm(PS(3, 0, 1), R("ONE", 0, 128), R("CUM", NJ, NJ + 1), True, True)
-            cp(LS(0), PS(4, 0, NJ))
+            cp(LS(0, 0, H1), PS(4, 0, H1))
+            cp(LS(0, H1, NJ), PS(6, H1, NJ))
             cp(LS(1), PS(5, 0, NJ))
-            cp(R("BI", 0, 1), PS(3, 0, 1))
-            ts(R("BJ", 0, 1), R("BI", 0, 1), 15, A.bitwise_and)
-            tt(R("THR", 0, 1), R("BJ", 0, 1), R("THI", 0, 1), A.add)
         else:
             dma("y", T.rl1[:, :], R("RLW", 0, 512))
             act(R("OU"), PS(4, 0, NJ), F.Copy)
             dma("s", T.up1[:, :], R("OU"))
-            act(R("OL"), PS(5, 0, NJ), F.Copy)
-            dma("s", T.lo1[:, :], R("OL"))
+            cp(R("OL"), PS(5, 0, NJ))
+            dma("y", T.lo1[:, :], R("OL"))
+
+    chain([i for i, o in enumerate(ops) if o["q"] == "g" and not o["free"]])
 
     def meet(x, z):
         if x[1] >= z[2] or z[1] >= x[2] or x[4] >= z[5] or z[4] >= x[5]:
@@ -495,26 +570,34 @@ def rank_program(g, core, T, topo):
                 acc.setdefault(x[0], []).append((i, x, isw))
 
     def delay(p, o, j):
-        if j not in o["deps"] and not p["post"]:
+        if j not in o["deps"] and not (p["post"] and o["pre"]):
             return 0.0
         return p["lat"] + (SAME if p["q"] == o["q"] else HOP)
 
     every = range(len(ops))
-    pred = [[(j, delay(ops[j], o, j)) for j in sorted(o["deps"] | o["order"])] for o in ops]
+    pred, sure, anc = [], [], []
+    for o in ops:
+        m, a = 0, 0
+        for j in o["deps"] | o["order"]:
+            m |= sure[j]
+            a |= anc[j] | 1 << j
+        pred.append([(j, delay(ops[j], o, j)) for j in sorted(o["deps"] | o["order"]) if not m >> j & 1])
+        sure.append(m | sum(1 << j for j in o["deps"] if not m >> j & 1))
+        anc.append(a)
     succ = [[] for o in ops]
     for i in every:
         for j, d in pred[i]:
             succ[j].append((i, d))
 
-    def judge(pri):
+    def judge(pri, pred, succ, t0):
         left = [len(p) for p in pred]
         ready = [i for i in every if not left[i]]
-        busy, at = {q: [] for q in Q}, {}
+        busy, at = {q: [] for q in Q}, [0.0] * len(ops)
         while ready:
             i = max(ready, key=lambda j: pri[j])
             ready.remove(i)
             c = ops[i]["cost"]
-            t = max([at[j] + ops[j]["cost"] + d for j, d in pred[i]] + [0.0])
+            t = max([at[j] + ops[j]["cost"] + d for j, d in pred[i]] + [t0[i]])
             bz = busy[ops[i]["q"]]
             k = len(bz)
             while k and bz[k - 1][1] > t:
@@ -528,41 +611,156 @@ def rank_program(g, core, T, topo):
                 left[j] -= 1
                 if not left[j]:
                     ready.append(j)
-        seq = sorted(every, key=lambda i: (at[i], i))
-        return sum(span(seq, sc) for sc in SCALES), seq, at
+        return at
 
-    def span(seq, scale):
-        at, q_at = {}, {q: 0.0 for q in Q}
+    def tighten(at):
+        back = judge([at[i] + ops[i]["cost"] for i in every], succ, pred, lats)
+        return judge([back[i] + ops[i]["cost"] for i in every], pred, succ, [0.0] * len(ops))
+
+    qn = ["vspgy".index(o["q"]) for o in ops]
+    lats = [o["lat"] for o in ops]
+    world = []
+    for k, m in enumerate(TIMES):
+        world.append(([o["costs"][k] for o in ops], [[(j, d * (m[5] if ops[j]["free"] else m[6])) for j, d in p] for p in pred],
+                      [[(j, d * (m[5] if ops[i]["free"] else m[6])) for j, d in succ[i]] for i in every]))
+
+    def worth(seq):
+        before, behind, q_last = [-1] * len(ops), [-1] * len(ops), [-1] * 5
         for i in seq:
-            o = ops[i]
-            t = q_at[o["q"]]
-            for j, d in pred[i]:
-                u = at[j] + (d * scale[2] if ops[j]["free"] else d)
-                if u > t:
-                    t = u
-            at[i] = q_at[o["q"]] = t + o["cost"] * (scale[0] if o["ix"] else scale[1] if o["q"] == "p" else 1.0)
-        return max(at[i] + ops[i]["lat"] for i in every)
+            j = before[i] = q_last[qn[i]]
+            if j >= 0:
+                behind[j] = i
+            q_last[qn[i]] = i
+        runs, total = [], 0.0
+        for c, pr, su in world:
+            end, why, rest = [0.0] * (len(ops) + 1), list(before), [0.0] * (len(ops) + 1)
+            for i in seq:
+                t = end[before[i]]
+                for j, d in pr[i]:
+                    u = end[j] + d
+                    if u > t:
+                        t, why[i] = u, j
+                end[i] = t + c[i]
+            for i in reversed(seq):
+                t = max(lats[i], rest[behind[i]])
+                for j, d in su[i]:
+                    u = rest[j] + d
+                    if u > t:
+                        t = u
+                rest[i] = t + c[i]
+            top = max(every, key=lambda i: end[i] + lats[i])
+            low = end[top] + lats[top] - 1.0
+            near = []
+            for i in every:
+                if end[i] - c[i] + rest[i] > low:
+                    near.extend((end[i] + d + rest[j], i, j) for j, d in su[i] + [(behind[i], 0.0), (-1, lats[i])])
+            near.sort(reverse=True)
+            runs.append((end, why, rest, near, top, low))
+            total += low + 1.0
+        return total, runs, before, behind
+
+    def change(now, pos, old, new):
+        total, a, b = -now[0], pos[old[0]], pos[old[-1]]
+        first, after = [None] * 5, [-1] * 5
+        for i in old:
+            if first[qn[i]] is None:
+                first[qn[i]] = now[2][i]
+            after[qn[i]] = now[3][i]
+        for (c, pr, su), (end, why, rest, near, top, val) in zip(world, now[1]):
+            keep, q_last = [end[i] for i in old], list(first)
+            for i in new:
+                t = end[q_last[qn[i]]]
+                for j, d in pr[i]:
+                    u = end[j] + d
+                    if u > t:
+                        t = u
+                t = end[i] = t + c[i]
+                q_last[qn[i]] = i
+                total += EPS * t
+                if t + lats[i] > val:
+                    val = t + lats[i]
+                for j, d in su[i]:
+                    if pos[j] > b and t + d + rest[j] > val:
+                        val = t + d + rest[j]
+            for q in range(5):
+                if first[q] is not None:
+                    val = max(val, end[q_last[q]] + rest[after[q]])
+            for v, i, j in near:
+                if v <= val:
+                    break
+                if pos[i] < a and (j < 0 or pos[j] > b):
+                    val = v
+            total += val - EPS * sum(keep)
+            for i, t in zip(old, keep):
+                end[i] = t
+        return total
 
     if not PLAN:
         pri = [o["cost"] + o["lat"] for o in ops]
         for i in reversed(every):
             for j, d in pred[i]:
                 pri[j] = max(pri[j], ops[j]["cost"] + d + pri[i])
-        best = judge(pri)
-        z = 12345
-        for _ in range(TRIES):
-            new = list(pri)
-            z = (z * 1103515245 + 12345) % 2147483648
-            a = z // 7 % len(ops)
-            z = (z * 1103515245 + 12345) % 2147483648
-            w_ = 1 + z // 11 % 6
-            z = (z * 1103515245 + 12345) % 2147483648
-            d = (z // 13 % 2001 - 1000) / 1000.0
-            for k in range(a, min(a + w_, len(ops))):
-                new[k] += 2.5 * d * abs(d)
-            got = judge(new)
-            if got[0] <= best[0]:
-                pri, best = new, got
+        at, now = judge(pri, pred, succ, [0.0] * len(ops)), None
+        for _ in range(TIGHT):
+            new = sorted(every, key=lambda i: (at[i], i))
+            got = worth(new)
+            if now is None or got[0] < now[0]:
+                seq, now = new, got
+            at = tighten(at)
+        best = (now[0], seq, now[1][0][0])
+        z = [12345]
+
+        def rnd_(k):
+            z[0] = (z[0] * 1103515245 + 12345) % 2147483648
+            return (z[0] >> 8) % k
+
+        held, seen = None, []
+        for it in range(TRIES):
+            if held is None:
+                held = []
+                for e, why, rest, near, i, low in now[1]:
+                    while why[i] >= 0:
+                        if qn[why[i]] == qn[i] and not anc[i] >> why[i] & 1:
+                            held.append((why[i], i))
+                        i = why[i]
+                pos = {i: k for k, i in enumerate(seq)}
+            if rnd_(4):
+                u, v = held[rnd_(len(held))]
+            else:
+                v = rnd_(len(ops))
+                u = now[1][0][1][v]
+                if u < 0 or qn[u] != qn[v] or anc[v] >> u & 1:
+                    continue
+            a, b = pos[u], pos[v]
+            far_ = rnd_(4)
+            if rnd_(2):
+                k = a - 1
+                while far_ > 1 and k >= 0 and not anc[v] >> seq[k] & 1:
+                    if qn[seq[k]] == qn[v]:
+                        a, far_ = k, far_ - 1
+                    k -= 1
+                up = [i for i in seq[a:b + 1] if i == v or anc[v] >> i & 1]
+            else:
+                k = b + 1
+                while far_ > 1 and k < len(seq) and not anc[seq[k]] >> u & 1:
+                    if qn[seq[k]] == qn[u]:
+                        b, far_ = k, far_ - 1
+                    k += 1
+                up = [i for i in seq[a:b + 1] if i != u and not anc[i] >> u & 1]
+            ups = set(up)
+            up += [i for i in seq[a:b + 1] if i not in ups]
+            seen.append((change(now, pos, seq[a:b + 1], up), a, b, up))
+            if len(seen) < BATCH and seen[-1][0] > -0.01:
+                continue
+            d, a, b, up = min(seen)
+            seen.clear()
+            if d <= SLACK * (1.0 - it / TRIES) * rnd_(100) / 100:
+                new = seq[:a] + up + seq[b + 1:]
+                got = worth(new)
+                e, c = got[1][0][0], world[0][0]
+                seq, now, held = sorted(new, key=lambda i: e[i] - c[i]), got, None
+                if now[0] < best[0]:
+                    best = (now[0], seq, e)
         PLAN.append(best)
     seq, at = PLAN[0][1], PLAN[0][2]
 

from concourse.bass import DstId, RemoteDMATransfer
from concourse.mybir import AluOpType as A, ActivationFunctionType as F

V, W, NG, NJ, NX, RO = 1568, 2048, 160, 98, 106, 3
SPARE = 2 * W - V
BIG = 1048576
CU = ((0, 28, 0), (28, 54, 1), (54, 78, 2), (78, 98, 3))
CW = ((0, 28, 6), (28, 56, 7), (56, 80, 0), (80, 98, 1))
JU, JA = 54, 56
H0 = 48
H1 = 48
SEG = ((6, 0, 4), (7, 4, 6), (2, 6, 8))
PGW = ((1, 1, 0, 0), (0, 0, 0, 0), (0, 0, 0, 0))
OFF = ((0,) * 6,) * 3
PV = ((0, 0, 0, 0), (0, 0, 0, 0), (0, 0, 0, 0))
WP = 8
GV = 66
KV = 9
KS = ((1, 9, 12), (3, 12, 16))
KSUM = ((0, 3), (9, 12), (3, 5), (5, 7), (12, 16), (7, 8), (8, 9))
HSV, SPE = 0, 1

HOP, SAME, REM, FIX = 0.10, 0.06, 8.0, {"v": 0.055, "s": 0.1}
TIMES = ((0.0009, 0.0005, 1.45, 3.5, 0, 1.0, 1.0, 0.3), (0.0011, 0.00058, 0.85, 2.3, 0, 1.1, 1.2, 0.2), (0.001, 0.00055, 1.75, 4.8, 0, 1.1, 1.0, 0.15))
YS = 3
TIGHT, TRIES, BATCH, SLACK, EPS = 8, 40000, 12, 0.2, 1e-4
PLAN = []

BF, FP, I32, U16 = "bfloat16", "float32", "int32", "uint16"
SB = {
    "X0": (W, BF), "X1": (W, BF), "X2": (W, BF), "M1U": (W, BF), "M1L": (W, BF), "M2U": (W, BF), "M2L": (W, BF),
    "C1U": (V, BF), "C1L": (V, BF), "C2U": (V, BF), "C2L": (V, BF), "EK": (128, FP), "KK": (128, BF),
    "YY": (W, BF), "ML": (V, BF), "WT": (V + 128, BF), "AU": (V, BF), "AL": (V, BF),
    "PT": (2 * W + 128, BF), "P2U": (W, BF), "P2L": (W, BF), "P4U": (V, BF), "P4L": (V, BF),
    "ULI": (196, I32), "ULA": (196, I32), "PP": (392, BF), "LS": (6 * NJ, U16), "THI": (4, I32), "THR": (4, FP),
    "THF": (4, FP), "BT": (4, FP), "C15": (8, BF), "JUNK": (424, BF),
    "RLI": (512, I32), "RLW": (648, FP), "SNI": (32, I32), "SNL": (32, U16),
    "SB0": (480, BF), "SB1": (480, BF), "SG": (960, BF), "B8": (16, BF), "GS0": (512, BF), "GS1": (512, BF),
    "UW": (16 * 144, BF), "BB": (3 * 144, BF), "II": (256, BF), "NII": (128, BF), "IDF": (128, FP), "ONE": (256, BF),
    "OB": (128, BF), "OBT": (128, BF), "NOB": (128, BF), "TRS": (128, BF),
    "TRI": (128, BF), "EV": (128, BF), "OD": (128, BF), "ZM": (128, BF), "SW": (128, BF),
    "T8": (48, BF), "ECC": (8, FP), "EC": (848, BF), "JT": (424, BF), "J16": (112, BF),
    "N1": (128, FP), "N0": (128, BF), "RST": (128, FP), "RS2": (576, BF), "DD": (576, BF),
    "DS": (576, BF), "C8": (8, BF), "DUM": (8, FP), "NW": (8, FP), "T16": (8, FP), "ENI": (8, I32), "ENL": (8, U16),
    "PI": (4, I32), "PJ": (4, I32), "COL": (8, FP), "GI": (480, FP),
    "DUS": (NJ, FP), "TU": (NJ, FP), "HB": (NJ, BF), "BAD": (112, BF), "CUM": (112, BF), "UPP": (NJ, FP),
    "TT": (NJ, FP), "HS": (112, BF), "FW": (112, BF), "ZW": (112, FP), "SC": (848, FP), "JL": (8, U16), "HJ": (16, BF),
    "OH": (128, BF), "QQ": (384, BF), "OJ": (128, BF), "LST": (16, U16), "HV": (16, FP), "CL": (128, U16),
    "WA": (128, BF), "GG": (W, BF), "AA": (W, BF), "QP": (128, BF), "CAB": (256, BF), "SM": (128, FP),
    "ST": (128, BF), "M2": (256, BF), "CP": (128, BF), "VUL": (8, U16), "NB": (8, FP),
    "XY": (8, FP), "RLL": (8, U16), "NV": (256, FP), "K4": (256, BF), "OU": (NJ, FP), "OL": (NJ, FP),
}
SCRATCH = {k: ("sbuf", [128, n], d) for k, (n, d) in SB.items()}
for _b in range(8):
    SCRATCH["ps%d" % _b] = ("psum", [128, 512], FP)
NDMA = 52
SEMAPHORES = ["cv", "cs", "cp", "cg", "arr0", "arr1", "snt0", "snt1", "dy0", "dy1", "dy2"] + ["d%d" % _i for _i in range(NDMA)]


def R(name, a=0, b=None, s=1, p0=0, p1=128):
    return (name, a, SB[name][0] if b is None else b, s, p0, p1)


def rank_program(g, core, T, topo):
    rank = T.rank_of(core)
    if rank is None:
        return
    cores = list(T.cores)
    n = len(cores)
    Q = {"v": g.vector, "s": g.scalar, "p": g.tensor, "g": g, "y": g.sync}
    ops = []
    ndma = [0]

    def ap(x):
        if not isinstance(x, tuple):
            return x
        if x[0] == "*":
            return ap(x[1]).indirect(ap(x[2]))
        if x[3] != 1:
            return T[x[0]][:, x[1]:x[2]:x[3]]
        if x[5] - x[4] < 128:
            return T[x[0]][x[4]:x[5], x[1]:x[2]]
        return T[x[0]][:, x[1]:x[2]]

    def IX(win, off):
        return ("*", win, off)

    def width(x):
        return 16 * width(x[2]) if x[0] == "*" else len(range(x[1], x[2], x[3]))

    def narrow(*xs):
        return all(x[0] in SB and SB[x[0]][1] in (BF, U16) for x in xs)

    def cost(q, outs, ins, f):
        o, i = outs[0], ins[0] if ins else None
        if q == "p":
            return [max(64, width(o)) * m[1] * (4 if SB[i[0]][1] == FP else 1) for m in TIMES]
        if q == "g":
            return [0.15 + 2 * width(o) * m[0] for m in TIMES]
        if o[0] == "*":
            return [FIX[q] + width(o) * m[3] * m[0] for m in TIMES]
        if i is not None and i[0] == "*":
            return [FIX[q] + width(o) * max(m[2], m[4] if f == 2 else 0) * m[0] for m in TIMES]
        if f is None:
            f = 0.5 if q == "v" and narrow(o, *[x for x in ins if isinstance(x, tuple) and width(x) > 1]) else 1
        return [FIX[q] + max(64, width(o) * f) * m[0] for m in TIMES]

    def add(q, fn, outs, ins, sem=None, inc=1, free=False, pre=None, f=None, lat=0.0, post=None, after=()):
        rd, wr = [], []
        for x in ins:
            if isinstance(x, tuple):
                rd.extend([x[1], x[2]] if x[0] == "*" else [x])
        for x in outs:
            if x[0] == "*":
                wr.append(x[1])
                rd.append(x[2])
            else:
                wr.append(x)
        c = [m[7] if inc else 0.5 for m in TIMES] if free else cost(q, outs, ins, f)
        ops.append({"q": q, "fn": fn, "rd": rd, "wr": wr, "sem": sem or "c" + q, "inc": inc, "free": free, "pre": pre, "post": post,
                    "cost": c[0], "costs": c, "lat": lat, "deps": set(after), "order": set()})
        return len(ops) - 1

    def cp(o, i):
        return add("v", lambda: g.vector.tensor_copy(ap(o), ap(i)), [o], [i])

    def tt(o, a, b, op):
        return add("v", lambda: g.vector.tensor_tensor(ap(o), ap(a), ap(b), op), [o], [a, b], f=1 if "ps" in (a[0][:2], b[0][:2]) else 2)

    def ts(o, a, s1, op0, s2=None, op1=None):
        if op1 is None:
            return add("v", lambda: g.vector.tensor_scalar(ap(o), ap(a), ap(s1), None, op0), [o], [a, s1])
        return add("v", lambda: g.vector.tensor_scalar(ap(o), ap(a), ap(s1), ap(s2), op0, op1), [o], [a, s1, s2])

    def scan(o, d0, d1, init, op0, op1):
        return add("v", lambda: g.vector.tensor_tensor_scan(ap(o), ap(d0), ap(d1), init, op0, op1), [o], [d0, d1])

    def mset(o, c):
        return add("v", lambda: g.vector.memset(ap(o), c), [o], [])

    def act(o, i, f=F.Identity, bias=0.0, scale=1.0, acc=None):
        if acc:
            return add("s", lambda: g.scalar.activation(ap(o), ap(i), f, bias=ap(bias), scale=ap(scale), accum_out=ap(acc)),
                       [o, acc], [i, bias, scale])
        return add("s", lambda: g.scalar.activation(ap(o), ap(i), f, bias=ap(bias), scale=ap(scale)), [o], [i, bias, scale])

    def mms(ms):
        def fn():
            return [g.tensor.matmul(ap(o), ap(l), ap(r), start, stop) for o, l, r, start, stop in ms][-1]
        i = add("p", fn, [m[0] for m in ms], [m[1] for m in ms] + [m[2] for m in ms], lat=0.05)
        ops[i]["costs"] = [sum(c) for c in zip(*[cost("p", [m[0]], [m[1]], None) for m in ms])]
        ops[i]["cost"] = ops[i]["costs"][0]
        return i

    def mm(o, l, r, start, stop):
        return mms([(o, l, r, start, stop)])

    def iota(o, pat, base, cm=0):
        if SB[o[0]][1] == I32:
            add("g", lambda: g.iota(ap(o), pat, base, cm), [o], [])
        else:
            add("g", lambda: g.iota(ap(o), pat, base, cm, allow_small_or_imprecise_dtypes=True), [o], [])

    def fill(o, c):
        iota(o, [[0, width(o)]], c)

    def sel(o, i, pat, op, base, cm, fillv=0.0):
        add("g", lambda: g.affine_select(ap(o), ap(i), pat, op, fillv, base, cm), [o], [i])

    def dma(q, o, i, pre=None, after=(), s=None):
        z = o if isinstance(o, tuple) else i
        if s is None:
            s = "d%d" % ndma[0]
            ndma[0] += 1
        return add(q, lambda: Q[q].dma_start(ap(o), ap(i)), [o] if isinstance(o, tuple) else [], [i], sem=s, inc=16, free=True, pre=pre,
                   lat=2.0 + width(z) * (0.0012 if narrow(z) else 0.0024) * (z[5] - z[4] + 32) / 160, after=after)

    def chain(ids):
        for a, b in zip(ids, ids[1:]):
            ops[b]["order"].add(a)

    def PS(b, a, e, s=1):
        return ("ps%d" % b, a, e, s, 0, 128)

    def BR(m, r):
        return R("BB", 144 * m + 15 - r, 144 * m + 143 - r)

    def UWs(r, i):
        return R("UW", 144 * r + 15 - i, 144 * r + 143 - i)

    def wrap(out, lhs, src, a, b, first=True, last=True):
        return [mms([(out, lhs(r), R(src, a + r, b, 16), first and r == 0, last and r == 15) for r in range(r0, r0 + WP)])
                for r0 in range(0, 16, WP)]

    def LS(k, a=0, b=NJ):
        return R("LS", NJ * k + a, NJ * k + b)

    def TRI0(t):
        return 8 * t * (t + 1)

    I_, NI_ = R("II", 0, 128), R("NII")

    d0 = dma("y", R("ULI", 0, 98), T.up[:, :])
    dma("s", R("ULI", 98, 196), T.lo[:, :])
    dx = dma("y", R("X0"), T.x[:, :])
    chain([d0, dx, dma("y", R("X1", 0, 16 * H0), T.x[:, 0:16 * H0]), dma("y", R("X1", 16 * H0, V), T.x[:, 16 * H0:V])])
    for b in ("M1U", "M1L", "M2U", "M2L", "YY"):
        dma("y", R(b, V, W), T.x[:, V:W], after=[dx])
    dma("y", R("WT", 0, V), T.w[:, :], after=[dx])
    dma("y", R("THI", 0, 1), T.th[:, :], after=[dx])
    dma("y", R("RLI"), T.rl[:, :], after=[dx])
    dma("y", R("SNI", 0, 30), T.snd[:, :], after=[dx])

    def diag(o, c):
        sel(o, R("ZM"), [[-1, 128]], A.not_equal, 0, 1, c)

    def block(m, lo_, hi_, c):
        sel(R("T8", 8 * m, 8 * m + 8), R("ZM", 0, 8), [[16, 8]], A.is_gt, lo_, -1, c)
        sel(R("BB", 144 * m + 15, 144 * m + 128, 16), R("T8", 8 * m, 8 * m + 8), [[16, 8]], A.is_ge, hi_, -1)

    chain([mset(R("ONE"), 1.0), mset(R("UW"), 0.0), mset(R("ZM"), 0.0), mset(R("BB"), 0.0)])
    iota(R("PI", 0, 1), [[0, 1]], 0, 1)
    iota(R("T16"), [[16, 8]], 0)
    sel(R("OBT"), R("ONE", 0, 128), [[-16, 8], [0, 16]], A.is_ge, 0, 1)
    sel(R("OB"), R("OBT"), [[16, 8], [0, 16]], A.is_ge, 15, -1)
    sel(R("II"), R("ONE"), [[0, 2], [-1, 128]], A.is_equal, 0, 1)
    sel(R("UW", 15, 2304, 16), R("ONE", 0, 144), [[-1, 16], [-16, 9]], A.is_equal, 0, 1)
    iota(R("GI"), [[1, 480]], V - 1792)
    for z, c in ((R("BAD", NJ, 112), 1), (R("CUM", 0, 1), 0), (R("HS", NJ, 112), 256), (R("HJ", 0, 8), 256), (R("FW", NJ, 112), SPARE)):
        fill(z, c)
    iota(R("C15", 0, 2), [[15, 2]], -15)
    block(1, 0, 1, 1.0)
    block(2, 2, 3, 1.0)
    diag(R("NII"), -1.0)
    ts(R("PJ", 0, 1), R("PI", 0, 1), 15, A.bitwise_and)
    ts(R("PJ", 1, 2), R("PI", 0, 1), 1, A.bitwise_and)
    cp(R("COL", 0, 2), R("PJ", 0, 2))
    act(R("COL", 2, 3), R("COL", 1, 2), bias=1.0, scale=-1.0)
    act(R("COL", 3, 4), R("COL", 1, 2), F.Copy, scale=1792.0)
    ts(R("COL", 4, 5), R("PJ", 0, 1), 8.0, A.is_ge)
    act(R("COL", 5, 6), R("COL", 4, 5), bias=1.0, scale=-1.0)
    act(R("PT", V, W), R("GI"), bias=R("COL", 3, 4), scale=R("COL", 2, 3))
    dma("y", R("P2U", V, W), R("PT", V, W))
    dma("y", R("P2L", V, W), R("PT", V, W))
    cp(R("THR", 0, 1), R("THI", 0, 1))
    cp(R("RLW", 0, 512), R("RLI"))
    cp(R("SNL", 0, 30), R("SNI", 0, 30))
    act(R("THF", 0, 1), R("THR", 0, 1), F.Copy)
    act(R("NOB"), R("OB"), F.Copy, scale=-256.0)
    act(R("B8", 0, 8), R("OB", 0, 128, 16), F.Copy, scale=256.0)
    act(R("B8", 8, 16), R("OB", 0, 128, 16), F.Copy, scale=-512.0)

    def late():
        block(0, 0, 15, 1.0)
        sel(R("TRS"), R("OB"), [[1, 128]], A.is_gt, 0, -1)
        sel(R("TRI"), R("OB"), [[1, 128]], A.is_ge, 0, -1)
        iota(R("JT"), [[0, 4], [2, NX]], -NX)
        diag(R("IDF"), 1.0)
        iota(R("N1"), [[2, 128]], 1)
        fill(R("RLW", 512, 648), 0)
        fill(R("WT", V, V + 128), 0)
        iota(R("KK"), [[0, 8], [-1, 16]], 0)
        sel(R("SW"), R("NOB"), [[0, 8], [1, 16]], A.is_ge, -KV, 0)
        iota(R("ENI"), [[16, 8]], 15)
        cp(R("ENL"), R("ENI"))
        iota(R("J16"), [[16, 112]], 0)
        iota(R("N0"), [[1, 128]], 0)
        fill(R("RST"), 4 * BIG)
        fill(R("RST", 0, 128, 16), -4 * BIG)
        sel(R("EV"), R("OB"), [[0, 64], [1, 2]], A.is_equal, 0, 0)
        sel(R("OD"), R("OB"), [[0, 64], [1, 2]], A.not_equal, 0, 0)
        fill(R("RS2"), 0)
        for t in range(8):
            fill(R("RS2", TRI0(t), TRI0(t) + 1), BIG)
        fill(R("PT", 2 * W, 2 * W + 128), 0)
        diag(R("K4", 0, 128), 4096.0)
        diag(R("K4", 128, 256), -4096.0)

    act(R("NW"), R("T16"), bias=R("COL", 0, 1))
    act(R("C8"), R("NW"), F.Copy, scale=1024.0)
    act(R("DUM"), R("NW"), bias=513.0)
    act(R("ECC"), R("NW"), bias=128.0, scale=256.0)
    for t in range(SEG[2][1]):
        act(R("EC", NX * t, NX * (t + 1)), R("ZM", 0, NX), bias=R("ECC", t, t + 1))

    ts(R("ULA"), R("ULI"), 511, A.bitwise_and)
    ts(R("PP", 0, 196), R("ULA"), -256.0, A.add)
    tt(R("PP", 196, 392), R("ULI"), R("PP", 0, 196), A.subtract)
    cp(R("LS", 0, 2 * NJ), R("ULI"))
    for r in range(8):
        for h in range(2):
            for parts in (((0, 0), (2, 98)), ((1, 196), (3, 294))):
                mms([(PS(r, h, 2 * NJ, 2), UWs(r + 8 * h, i), R("PP", a, a + NJ), i == 0, i == 3) for i, a in parts])
        act(R("PT", r, V, 8), PS(r, 0, 2 * NJ), F.Copy)

    for rnd in range(RO):
        X, XO = "X%d" % rnd, "X%d" % ((rnd + 1) % RO)
        L0 = 0 if rnd == 0 else W
        last = rnd == RO - 1
        steps, pgs, diffs, vs, lists = [], [], [], [], {}

        def ahead(k):
            if k in lists and rnd:
                ops[steps[-1]]["order"].add(lists[k])

        def step(o, win, own, k, a, b):
            steps.append(tt(R(o, 16 * a, 16 * b), IX(R(win), LS(k, a, b)), R(own, 16 * a, 16 * b), A.max))
            if rnd and win == X:
                ops[-1]["pre"] = ("arr%d" % (rnd - 1), 16)

        def shared(o, win, k, a, b, c):
            if a < b:
                gb = "GS%d" % (k % 2)
                act(R(gb, 0, 16 * (b - a)), IX(R(win), LS(k, a, b)), F.Copy)
                if rnd and win == X:
                    ops[-1]["pre"] = ("arr%d" % (rnd - 1), 16)
                mm(PS(c, 0, 16 * (b - a)), I_, R(win, 16 * a, 16 * b), True, True)
                steps.append(tt(R(o, 16 * a, 16 * b), PS(c, 0, 16 * (b - a)), R(gb, 0, 16 * (b - a)), A.max))

        def step2(o, win, own, k, twin, halves, c):
            e, e2 = NJ - OFF[rnd][k], NJ - OFF[rnd][k + 2]
            for h, (a, b) in enumerate(halves + ((e, NJ),)):
                if h < len(halves):
                    b = min(b, e)
                    step(o, win, own, k, a, b)
                else:
                    shared(o, win, k, a, b, c)
                b = min(b, e2)
                if h < len(halves) - 1:
                    dma("y", R(twin, 16 * a, 16 * b), R(o, 16 * a, 16 * b))
                elif a < b:
                    sel(R(twin, 16 * a, 16 * b), R(o, 16 * a, 16 * b), [[0, 16 * (b - a)]], A.is_ge, 0, 0)

        def pg(o, win, k, w0, parts, m, banks):
            for (a, b), c in zip(parts, banks):
                e = min(b, NJ - PV[rnd][k])
                pgs.append(act(R(o, 16 * a, 16 * e), IX(R(win, w0, w0 + W), LS(k, a, e)), F.Copy))
                if e < b:
                    cp(R(o, 16 * e, 16 * b), IX(R(win, w0, w0 + W), LS(k, e, b)))
                if PGW[rnd][k]:
                    wrap(PS(c, a, b), lambda r: BR(m, r), o, 16 * a, 16 * b)
                    cp(LS(k + 2, a, b), PS(c, a, b))
            if not PGW[rnd][k]:
                wrap(PS(banks[0], 0, NJ), lambda r: BR(m, r), o, 0, V)
                lists[k] = cp(LS(k + 2), PS(banks[0], 0, NJ))

        def far(buf, out, a, b, c, scale=1.0):
            diffs.append(mm(PS(c, 0, 16 * (b - a)), I_, R(buf, 16 * a, 16 * b), False, True))
            pgs.append(act(R(out, 16 * a, 16 * b), PS(c, 0, 16 * (b - a)), F.Abs, scale=scale))

        def negw(a, b, c):
            mm(PS(c, 0, 16 * (b - a)), NI_, R("WT", 16 * a, 16 * b), True, False)

        up_, dn_ = ((0, H0), (H0, NJ)), ((H0, NJ), (0, H0))
        step2("M1U", X, XO, 0, "C1U", ((0, H1), (H1, NJ)) if rnd else up_, 1)
        whole = ((0, NJ),)
        pg("P2U", "PT", 0, 0, dn_ if PGW[rnd][0] else ((0, H1), (H1, NJ)), 1, (0, 1))
        step2("M1L", X, XO, 1, "C1L", up_, 3)
        ahead(0)
        pg("P2L", "PT", 1, L0, dn_ if PGW[rnd][1] else whole, 2, (2, 3))
        DH, HL = PS(5, 128, 128 + NJ), PS(4, 128, 128 + NJ)
        wrap(HL, lambda r: UWs(2, r), "PT", L0, L0 + V)
        act(R("HB"), HL, F.Copy)
        wrap(DH, lambda r: UWs(0, r), "PT", 0, V, True, False)
        mm(DH, NI_, R("HB"), False, True)
        d3_ = ((H0, NJ), (NJ - H0, H0), (0, NJ - H0)) if 2 * H0 > NJ else dn_
        step2("M2U", "M1U", "C1U", 2, "C2U", d3_, 4)
        ahead(1)
        pg("P4U", "P2U", 2, 0, up_ if PGW[rnd][2] else whole, 1, (1, 3))
        step2("M2L", "M1L", "C1L", 3, "C2L", d3_, 7)
        ahead(2)
        pg("P4L", "P2L", 3, 0, up_ if PGW[rnd][3] else whole, 2, (4, 5))
        if rnd == 0:
            late()
            twin = max(i for i, o in enumerate(ops) if o["q"] == "y")
            dma("y", R("X2", 0, V), T.x[:, 0:V], after=[twin])
            dma("y", R("PT", W, 2 * W), R("PT", 0, W), after=[twin])
        else:
            nb = R("CUM", NJ, NJ + 1)
            mms([(PS(2, 256, 258), I_, R("C15", 0, 2), True, False), (PS(2, 256, 257), R("ONE", 0, 128), nb, False, False),
                 (PS(2, 256, 257), R("ONE", 0, 128), nb, False, False), (PS(2, 257, 258), R("ONE", 0, 128), nb, False, False),
                 (PS(2, 257, 258), R("IDF"), R("THF", 0, 1), False, True)])
            pgs.append(act(R("BT", 0, 1), PS(2, 256, 257), bias=12582912.0, scale=1.0 / 32))
            pgs.append(act(R("BT", 1, 2), R("BT", 0, 1), bias=201326592.0, scale=-16.0))
            pgs.append(act(R("THR", 0, 1), PS(2, 257, 258), bias=R("BT", 1, 2)))
        for a, b, c in CU:
            negw(a, b, c)
            if a < NJ - OFF[rnd][4]:
                step("YY", "M2U", "C2U", 4, a, b)
            else:
                shared("YY", "M2U", 4, a, b, 7)
            far("YY", "AU", a, b, c)
        ahead(3)
        if not last:
            pgs.append(act(R("SG", 0, 480), IX(R("YY", 0, V), R("SNL", 0, 30)), F.Copy, scale=R("COL", 5, 6)))
        for k, (a, b, c) in enumerate(CW):
            negw(a, b, c)
            step("ML", "M2L", "C2L", 5, a, b)
            far("ML", "AL", a, b, c)
            if k == 0:
                wrap(PS(4, 0, JU), lambda r: BR(0, r), "AU", 0, 16 * JU)
                wrap(PS(4, JU, NJ), lambda r: BR(0, r), "AU", 16 * JU, V)
        ts(R("TU"), PS(4, 0, NJ), -1.0, A.mult, R("THR", 0, 1), A.add)
        act(R("DUS"), PS(4, 0, NJ), F.Copy)
        wrap(PS(5, 0, JA), lambda r: BR(0, r), "AL", 0, 16 * JA)
        wrap(PS(5, JA, NJ), lambda r: BR(0, r), "AL", 16 * JA, V)
        for c, a, b in SEG[:2]:
            mm(PS(c, 0, NX * (b - a)), I_, R("EC", NX * a, NX * b), True, False)
        chain(steps)
        chain(pgs)
        chain(diffs)
        for p in range(8, 128, 16):
            dma("s" if p < 16 * YS else "y", R("YY", 0, V, 1, p, p + 8), R("ML", 0, V, 1, p, p + 8), s="dy%d" % rnd)
        if last:
            dma("y", T.y[:, :], R("YY", 0, V))
        else:
            ts(R("SG", 480, 960), IX(R("ML"), R("SNL", 0, 30)), R("COL", 4, 5), A.mult)
            if SPE:
                mm(PS(3, 0, 480), I_, R("SG", 0, 480), True, SPE == 1)
            if SPE == 2:
                mm(PS(3, 0, 480), I_, R("SG", 480, 960), False, True)
            for a, b in ((0, 2 * NG), (2 * NG, 3 * NG)):
                if SPE == 2:
                    act(R("SB%d" % rnd, a, b), PS(3, a, b), F.Copy)
                    continue
                vs.append(tt(R("SB%d" % rnd, a, b), PS(3, a, b) if SPE else R("SG", a, b), R("SG", 480 + a, 480 + b), A.add))
        vs.append(tt(R("BAD", 0, NJ), PS(5, 0, NJ), R("TU"), A.is_gt))
        vs += [scan(R("CUM", 1, NX + 1), R("BAD", 0, NX), R("BAD", 0, NX), 0.0, A.add, A.max),
              tt(R("UPP"), PS(5, 0, NJ), R("DUS"), A.is_le), tt(R("TT"), DH, R("UPP"), A.mult)]
        if HSV:
            tt(R("HS", 0, NJ), HL, R("TT"), A.add)
        else:
            mms([(PS(1, 0, NJ), I_, R("HB"), True, False), (PS(1, 0, NJ), R("IDF"), R("TT"), False, True)])
            act(R("HS", 0, NJ), PS(1, 0, NJ), F.Copy)
        for c, a, b in SEG[:2]:
            mms([(PS(c, NX * t, NX * (t + 1)), R("NOB"), R("CUM", 1, NX + 1), False, t == b - a - 1) for t in range(b - a)])
        mm(PS(SEG[2][0], 0, NX), R("NOB"), R("CUM", 1, NX + 1), True, True)
        mms([(PS(0, 0, NX), R("TRI"), R("BAD", 0, NX), True, False), (PS(0, 0, NX), R("TRS"), R("BAD", 0, NX), False, False)])
        mms([(PS(0, 0, NX), R("OB"), R("CUM", 0, NX), False, False), (PS(0, 0, NX), R("OB"), R("CUM", 0, NX), False, True)])
        chain(vs + [scan(R("SC", NX * a, NX * b), R("JT", 0, NX * (b - a)), PS(c, 0, NX * (b - a)), 1000.0, A.min, A.max)
                    for c, a, b in SEG[:2]])
        c, a, b = SEG[2]
        for t in range(a, b):
            act(R("JUNK", NX * (t - a), NX * (t - a + 1)), PS(c, 0, NX), F.Sign, bias=R("ECC", t, t + 1), acc=R("SC", NX * t + NX - 1, NX * t + NX))
        act(R("ZW", 0, NX), PS(0, 0, NX), F.Copy)
        ts(R("JL"), R("SC", NX - 1, 848, NX), 0.5, A.mult, NX / 2, A.add)
        act(R("HJ", 8, 16), R("SC", NX - 1, 848, NX), bias=8.0 * NX, scale=8.0)
        for c, k0, k1 in KS:
            mm(PS(c, 0, 128 * (k1 - k0)), R("ZM"), R("WT", 0, 128 * (k1 - k0)), True, False)
        mm(PS(4, 256, 384), I_, R("KK"), True, False)
        tt(R("OH"), IX(R("ZW", 0, NX), R("JL")), R("N1"), A.is_equal)
        act(R("QQ", 128, 256), R("OH"), F.Copy, scale=R("COL", 0, 1))
        tt(R("QQ", 0, 128), IX(R("HS", 0, NX), R("JL")), R("OH"), A.mult)
        mm(PS(5, 128, 144), I_, R("HJ"), True, False)
        wrap(PS(5, 128, 144), lambda r: BR(0, r), "QQ", 0, 256, False, True)
        act(R("FW", 0, NJ), R("UPP"), bias=float(W), scale=-float(W))
        act(R("OJ"), IX(R("J16", 0, NX), R("JL")), F.Copy)
        tt(R("QQ", 256, 384), IX(R("FW", 0, NX), R("JL")), R("OH"), A.mult)
        cp(R("LST"), PS(5, 128, 144))
        hl, vl = R("LST", 0, 8), R("LST", 8, 16)
        if not last:
            def send(rnd, ds):
                tr = []
                for d in ds:
                    dst = cores[(rank + d) % n]
                    rid, pid = topo.addr(dst, core)
                    e = topo.engines(core, dst)
                    hlf = len(e) // 2
                    e = e[:hlf] if d == 1 else (e[hlf:2 * hlf] if d == 2 else e)
                    tr.append(RemoteDMATransfer(
                        dst_ids=[DstId(rid=rid, pnc=pid)], dma_engine_mask=sum(1 << x for x in e), remote_sem=T.sem["arr%d" % rnd],
                        src=ap(R("SB%d" % rnd, NG * (d - 1), NG * d)), dst=ap(R("X%d" % (rnd + 1), V + NG * (d - 1), V + NG * d))))
                g.remote_dma_fused(tr, local_sem=T.sem["snt%d" % rnd])
            ids = []
            for ds in ((1, 2), (3,)):
                z = R("SB%d" % rnd, NG * (ds[0] - 1), NG * ds[-1])
                ids.append(add("g", lambda rnd=rnd, ds=ds: send(rnd, ds), [], [z], free=True, inc=0, lat=REM, post="arr%d" % rnd))
            chain(ids)
        cp(R("CL"), IX(R("RLW"), hl))
        act(R("WA"), IX(R("WT"), vl), F.Copy)
        cp(R("GG", 0, 16 * GV), IX(R("YY"), R("CL", 0, GV)))
        act(R("GG", 16 * GV, W), IX(R("YY"), R("CL", GV, 128)), F.Copy)
        if not last:
            for b in ("M1U", "M1L", "M2U", "M2L", "YY"):
                dma("y", R(b, V, W), R("X%d" % (rnd + 1), V, W), pre=("arr%d" % rnd, 16))
        ids = []
        mm(PS(0, 0, 128), I_, R("WA"), True, True)
        for c, k0, k1 in KS:
            mms([(PS(c, 128 * (k - k0), 128 * (k - k0 + 1)), I_, R("WA"), False, False) for k in range(k0, k1)])
            ids.append(mms([(PS(c, 128 * (k - k0), 128 * (k - k0 + 1)), NI_, R("GG", k, W, 16), False, k == k1 - 1) for k in range(k0, k1)]))
        mm(PS(4, 256, 384), R("WA"), R("SW"), False, False)
        ids.append(mms([(PS(4, 256 + k, 384, 16), R("GG", k, W, 16), R("B8", 0, 8), False, False) for k in range(KV)]))
        chain(ids)
        act(R("QP"), IX(R("RLW"), hl), bias=191.5009765625, scale=1.0 / 512)
        chain([tt(R("AA", 128 * k, 128 * k + 128), PS(0, 0, 128), R("GG", k, W, 16), A.max) for k in range(KV)])
        for c, k0, k1 in KS:
            act(R("AA", 128 * k0, 128 * k1), PS(c, 0, 128 * (k1 - k0)), F.Abs)
        for k0, k1 in KSUM:
            mms([(PS(4, 256 + k, 384, 16), R("AA", 128 * k, 128 * k + 128), R("B8", 8, 16) if k < KV else R("NOB", 0, 128, 16), False,
                  k == KSUM[-1][1] - 1) for k in range(k0, k1)])
        act(R("CAB", 128, 256), R("QP"), bias=-98048.0, scale=512.0)
        act(R("HV"), PS(5, 128, 144), F.Copy)
        scan(R("SM"), R("RST"), PS(4, 256, 384), 0.0, A.min, A.max)
        cp(R("EK"), PS(4, 256, 384))
        st = tt(R("ST"), IX(R("SM"), R("ENL")), R("EK"), A.is_equal)
        mms([(PS(5, 256, 384), NI_, R("N0"), True, False), (PS(5, 256, 384), R("NOB"), R("QQ", 0, 128), False, True)])
        mm(PS(0, 0, 256), R("ST"), R("II"), True, True)
        mm(PS(7, 8, 16), R("IDF"), R("HV", 8, 16), True, False)
        wrap(PS(7, 8, 16), lambda r: BR(0, r), "QQ", 256, 384, False, True)
        chain([st, tt(R("CAB", 0, 128), IX(R("RLW"), hl), R("CAB", 128, 256), A.subtract)])
        act(R("NB"), R("HV", 0, 8), bias=-67108864.0, scale=262144.0)
        tt(R("M2"), PS(0, 0, 256), R("CAB"), A.mult)
        mms([(PS(1, 0, 128), R("EV"), R("M2", 0, 128), True, False), (PS(1, 0, 128), R("OD"), R("M2", 128, 256), False, True)])
        mms([(PS(2, 0, 256), R("ST"), R("K4"), True, False), (PS(2, 0, 128), I_, R("OJ"), False, False),
             (PS(2, 0, 128), R("OB"), R("QQ", 128, 256), False, False), (PS(2, 0, 128), R("NOB"), R("ONE", 0, 128), False, False),
             (PS(2, 128, 256), I_, R("CAB", 0, 128), False, False), (PS(2, 128, 256), I_, R("CAB", 128, 256), False, True)])
        cp(R("VUL"), PS(7, 8, 16))
        for t in range(8):
            act(R("DD", TRI0(t), TRI0(t + 1)), PS(5, 256, 256 + 16 * (t + 1)), F.Abs, bias=R("NB", t, t + 1), scale=1024.0)
        act(R("NV"), PS(2, 0, 256), F.Copy)
        ids = [scan(R("DS"), R("RS2"), R("DD"), 0.0, A.max, A.min), cp(R("CP"), PS(1, 0, 128))]
        ids.append(cp(IX(R("PT"), R("VUL")), R("CP")))
        mms([(PS(3, 0, 8), I_, R("C8"), True, False), (PS(3, 0, 8), R("IDF"), R("HV", 0, 8), False, False)])
        mms([(PS(3, t, t + 1), NI_, R("DS", TRI0(t + 1) - 1, TRI0(t + 1)), False, t == 7) for t in range(8)])
        if last:
            ws = wrap(PS(4, 0, NJ), lambda r: BR(1, r), "PT", 0, V)
        else:
            ws = wrap(PS(4, 0, H1), lambda r: BR(1, r), "PT", 0, 16 * H1) + wrap(PS(6, H1, NJ), lambda r: BR(1, r), "PT", 16 * H1, V)
        chain(ws + wrap(PS(5, 0, NJ), lambda r: BR(2, r), "PT", W, W + V))
        ids += [tt(R("XY"), PS(3, 0, 8), R("DUM"), A.min), cp(R("RLL"), R("XY"))]
        tt(IX(R("RLW"), R("RLL")), R("NV", 0, 128), R("NV", 128, 256), A.max)
        if not last:
            cp(LS(0, 0, H1), PS(4, 0, H1))
            cp(LS(0, H1, NJ), PS(6, H1, NJ))
            cp(LS(1), PS(5, 0, NJ))
        else:
            dma("y", T.rl1[:, :], R("RLW", 0, 512))
            act(R("OU"), PS(4, 0, NJ), F.Copy)
            dma("s", T.up1[:, :], R("OU"))
            cp(R("OL"), PS(5, 0, NJ))
            dma("y", T.lo1[:, :], R("OL"))

    chain([i for i, o in enumerate(ops) if o["q"] == "g" and not o["free"]])

    def meet(x, z):
        if x[1] >= z[2] or z[1] >= x[2] or x[4] >= z[5] or z[4] >= x[5]:
            return False
        return not (x[3] == z[3] > 1 and (x[1] - z[1]) % x[3])

    acc, posts = {}, {}
    for i, o in enumerate(ops):
        for lst, isw in ((o["rd"], False), (o["wr"], True)):
            for x in lst:
                for (j, z, w_) in acc.get(x[0], ()):
                    p = ops[j]
                    if x[0][:2] == "ps" and p["q"] != o["q"]:
                        o["deps"].add(j)
                    elif x[0][:2] == "ps" and o["q"] == "p":
                        o["order"].add(j)
                    elif (w_ or isw) and meet(x, z):
                        o["deps"].add(j)
        if o["pre"]:
            o["order"].add(posts[o["pre"][0]])
        if o["post"]:
            posts[o["post"]] = i
        for lst, isw in ((o["rd"], False), (o["wr"], True)):
            for x in lst:
                if x[0][:2] == "ps" and o["q"] == "p":
                    acc[x[0]] = [e for e in acc.get(x[0], ()) if ops[e[0]]["q"] != "p"]
                acc.setdefault(x[0], []).append((i, x, isw))

    def delay(p, o, j):
        if j not in o["deps"] and not (p["post"] and o["pre"]):
            return 0.0
        return p["lat"] + (SAME if p["q"] == o["q"] else HOP)

    every = range(len(ops))
    pred, sure, anc = [], [], []
    for o in ops:
        m, a = 0, 0
        for j in o["deps"] | o["order"]:
            m |= sure[j]
            a |= anc[j] | 1 << j
        pred.append([(j, delay(ops[j], o, j)) for j in sorted(o["deps"] | o["order"]) if not m >> j & 1])
        sure.append(m | sum(1 << j for j in o["deps"] if not m >> j & 1))
        anc.append(a)
    succ = [[] for o in ops]
    for i in every:
        for j, d in pred[i]:
            succ[j].append((i, d))

    def judge(pri, pred, succ, t0):
        left = [len(p) for p in pred]
        ready = [i for i in every if not left[i]]
        busy, at = {q: [] for q in Q}, [0.0] * len(ops)
        while ready:
            i = max(ready, key=lambda j: pri[j])
            ready.remove(i)
            c = ops[i]["cost"]
            t = max([at[j] + ops[j]["cost"] + d for j, d in pred[i]] + [t0[i]])
            bz = busy[ops[i]["q"]]
            k = len(bz)
            while k and bz[k - 1][1] > t:
                k -= 1
            while k < len(bz) and bz[k][0] < t + c - 1e-9:
                t = max(t, bz[k][1])
                k += 1
            bz.insert(k, (t, t + c))
            at[i] = t
            for j, d in succ[i]:
                left[j] -= 1
                if not left[j]:
                    ready.append(j)
        return at

    def tighten(at):
        back = judge([at[i] + ops[i]["cost"] for i in every], succ, pred, lats)
        return judge([back[i] + ops[i]["cost"] for i in every], pred, succ, [0.0] * len(ops))

    qn = ["vspgy".index(o["q"]) for o in ops]
    lats = [o["lat"] for o in ops]
    world = []
    for k, m in enumerate(TIMES):
        world.append(([o["costs"][k] for o in ops], [[(j, d * (m[5] if ops[j]["free"] else m[6])) for j, d in p] for p in pred],
                      [[(j, d * (m[5] if ops[i]["free"] else m[6])) for j, d in succ[i]] for i in every]))

    def worth(seq):
        before, behind, q_last = [-1] * len(ops), [-1] * len(ops), [-1] * 5
        for i in seq:
            j = before[i] = q_last[qn[i]]
            if j >= 0:
                behind[j] = i
            q_last[qn[i]] = i
        runs, total = [], 0.0
        for c, pr, su in world:
            end, why, rest = [0.0] * (len(ops) + 1), list(before), [0.0] * (len(ops) + 1)
            for i in seq:
                t = end[before[i]]
                for j, d in pr[i]:
                    u = end[j] + d
                    if u > t:
                        t, why[i] = u, j
                end[i] = t + c[i]
            for i in reversed(seq):
                t = max(lats[i], rest[behind[i]])
                for j, d in su[i]:
                    u = rest[j] + d
                    if u > t:
                        t = u
                rest[i] = t + c[i]
            top = max(every, key=lambda i: end[i] + lats[i])
            low = end[top] + lats[top] - 1.0
            near = []
            for i in every:
                if end[i] - c[i] + rest[i] > low:
                    near.extend((end[i] + d + rest[j], i, j) for j, d in su[i] + [(behind[i], 0.0), (-1, lats[i])])
            near.sort(reverse=True)
            runs.append((end, why, rest, near, top, low))
            total += low + 1.0
        return total, runs, before, behind

    def change(now, pos, old, new):
        total, a, b = -now[0], pos[old[0]], pos[old[-1]]
        first, after = [None] * 5, [-1] * 5
        for i in old:
            if first[qn[i]] is None:
                first[qn[i]] = now[2][i]
            after[qn[i]] = now[3][i]
        for (c, pr, su), (end, why, rest, near, top, val) in zip(world, now[1]):
            keep, q_last = [end[i] for i in old], list(first)
            for i in new:
                t = end[q_last[qn[i]]]
                for j, d in pr[i]:
                    u = end[j] + d
                    if u > t:
                        t = u
                t = end[i] = t + c[i]
                q_last[qn[i]] = i
                total += EPS * t
                if t + lats[i] > val:
                    val = t + lats[i]
                for j, d in su[i]:
                    if pos[j] > b and t + d + rest[j] > val:
                        val = t + d + rest[j]
            for q in range(5):
                if first[q] is not None:
                    val = max(val, end[q_last[q]] + rest[after[q]])
            for v, i, j in near:
                if v <= val:
                    break
                if pos[i] < a and (j < 0 or pos[j] > b):
                    val = v
            total += val - EPS * sum(keep)
            for i, t in zip(old, keep):
                end[i] = t
        return total

    if not PLAN:
        pri = [o["cost"] + o["lat"] for o in ops]
        for i in reversed(every):
            for j, d in pred[i]:
                pri[j] = max(pri[j], ops[j]["cost"] + d + pri[i])
        at, now = judge(pri, pred, succ, [0.0] * len(ops)), None
        for _ in range(TIGHT):
            new = sorted(every, key=lambda i: (at[i], i))
            got = worth(new)
            if now is None or got[0] < now[0]:
                seq, now = new, got
            at = tighten(at)
        best = (now[0], seq, now[1][0][0])
        z = [12345]

        def rnd_(k):
            z[0] = (z[0] * 1103515245 + 12345) % 2147483648
            return (z[0] >> 8) % k

        held, seen = None, []
        for it in range(TRIES):
            if held is None:
                held = []
                for e, why, rest, near, i, low in now[1]:
                    while why[i] >= 0:
                        if qn[why[i]] == qn[i] and not anc[i] >> why[i] & 1:
                            held.append((why[i], i))
                        i = why[i]
                pos = {i: k for k, i in enumerate(seq)}
            if rnd_(4):
                u, v = held[rnd_(len(held))]
            else:
                v = rnd_(len(ops))
                u = now[1][0][1][v]
                if u < 0 or qn[u] != qn[v] or anc[v] >> u & 1:
                    continue
            a, b = pos[u], pos[v]
            far_ = rnd_(4)
            if rnd_(2):
                k = a - 1
                while far_ > 1 and k >= 0 and not anc[v] >> seq[k] & 1:
                    if qn[seq[k]] == qn[v]:
                        a, far_ = k, far_ - 1
                    k -= 1
                up = [i for i in seq[a:b + 1] if i == v or anc[v] >> i & 1]
            else:
                k = b + 1
                while far_ > 1 and k < len(seq) and not anc[seq[k]] >> u & 1:
                    if qn[seq[k]] == qn[u]:
                        b, far_ = k, far_ - 1
                    k += 1
                up = [i for i in seq[a:b + 1] if i != u and not anc[i] >> u & 1]
            ups = set(up)
            up += [i for i in seq[a:b + 1] if i not in ups]
            seen.append((change(now, pos, seq[a:b + 1], up), a, b, up))
            if len(seen) < BATCH and seen[-1][0] > -0.01:
                continue
            d, a, b, up = min(seen)
            seen.clear()
            if d <= SLACK * (1.0 - it / TRIES) * rnd_(100) / 100:
                new = seq[:a] + up + seq[b + 1:]
                got = worth(new)
                e, c = got[1][0][0], world[0][0]
                seq, now, held = sorted(new, key=lambda i: e[i] - c[i]), got, None
                if now[0] < best[0]:
                    best = (now[0], seq, e)
        PLAN.append(best)
    seq, at = PLAN[0][1], PLAN[0][2]

    used = set()
    for o in ops:
        used |= o["deps"]
    cnt = {}
    for i in seq:
        o = ops[i]
        o["sig"] = o["inc"] > 0 and (i in used or o["free"])
        if o["sig"]:
            cnt[o["sem"]] = cnt.get(o["sem"], 0) + o["inc"]
            o["val"] = cnt[o["sem"]]
    for o in ops:
        if o["free"] and o["sig"]:
            o["val"] = cnt[o["sem"]]
    known = {q: {} for q in Q}
    waited = {}
    for i in seq:
        o = ops[i]
        kn = known[o["q"]]
        need = {}
        for j in o["deps"]:
            p = ops[j]
            if p["val"] > need.get(p["sem"], (0, 0))[0]:
                need[p["sem"]] = (p["val"], j)
        for s, (val, j) in sorted(need.items(), key=lambda z: -at[z[1][1]]):
            if kn.get(s, 0) < val:
                Q[o["q"]].wait_ge(T.sem[s], val)
                waited[s] = max(waited.get(s, 0), val)
                kn[s] = val
                for s2, v2 in ops[j]["kn"].items():
                    if kn.get(s2, 0) < v2:
                        kn[s2] = v2
        if o["pre"] and kn.get(o["pre"][0], 0) < o["pre"][1]:
            Q[o["q"]].wait_ge(T.sem[o["pre"][0]], o["pre"][1])
            kn[o["pre"][0]] = o["pre"][1]
        o["kn"] = dict(kn)
        ins = o["fn"]()
        if o["sig"]:
            ins.then_inc(T.sem[o["sem"]], o["inc"])
    cnt["snt0"] = cnt["snt1"] = 16
    for s, val in cnt.items():
        if waited.get(s, 0) < val:
            g.wait_ge(T.sem[s], val)
